import numpy as np, ml_dtypes
CORES = [10,34,74,98]
N = 4
import mx_ref
BF = ml_dtypes.bfloat16
def cols(t, e):
    v = np.concatenate([t.reshape(128, -1, 4), np.zeros((128, 1, 4), BF)], axis=1)
    return np.ascontiguousarray(v[:, e]).reshape(128, -1)
def tile(rs):
    return np.stack(rs, axis=2).reshape(128, -1).astype(BF)
def cut(t, i, w=512):
    return t[:, w * i:w * i + w]
def f(rng, *shape):
    return mx_ref.flush((rng.standard_normal(shape, dtype=np.float32) * np.exp2(rng.integers(-2, 3, shape[:-1] + (1,)))).astype(BF))
def wide(rng, *shape, cols=0):
    v = rng.standard_normal(shape, dtype=np.float32) * np.exp2(rng.integers(-12, 13, shape)).astype(np.float32)
    if cols: v *= np.repeat(np.exp2(rng.integers(-cols, cols + 1, shape[:-2] + (1, shape[-1] // 4))) * (rng.random(shape[:-2] + (1, shape[-1] // 4)) > 0.0625), 4, axis=-1).astype(np.float32)
    return mx_ref.flush(v.astype(BF))
T, ST = 512, 128
def flags(rng, n, new):
    s = np.zeros((N, T), bool)
    for r in range(N):
        s[r, 0] = new[r] > 0
        s[r, 1 + rng.permutation(T - 1)[:int(n[r]) - int(new[r])]] = True
    return s
def borders(rng):
    new = rng.integers(0, 2, N); new[0] = 1
    return new
def make(rng, s, far=2, spread=False):
    t = np.zeros((128, 128, 4), np.float32); t[:, :16] = rng.standard_normal((128, 16, 4), dtype=np.float32)
    if spread: t[64:] = 0
    t = mx_ref.flush(t.reshape(128, 512).astype(BF))
    k = (rng.integers(0, 16) + np.cumsum(s.reshape(-1) * rng.integers(1, 16, N * T))) % 16
    c = t.astype(np.float32).reshape(128, 128, 4)[:, k] + rng.standard_normal((128, N * T, 4), dtype=np.float32) * np.float32(0.125)
    if spread: c[64:] = wide(rng, 64, 4 * N * T).astype(np.float32).reshape(64, N * T, 4)
    c = c * np.exp2(rng.integers(-far, far + 1, (N * T, 1))).astype(np.float32)
    x = np.ascontiguousarray(c.reshape(128, N, 4 * T).transpose(1, 0, 2)).astype(BF)
    return {"x": mx_ref.flush(x), "p": np.stack([t] * N), "a": f(rng, N, 128, 2048), "w": f(rng, N, 128, 512), "v": f(rng, N, 128, 512)}
def setup_inputs(rng):
    return make(rng, flags(rng, rng.integers(1, ST + 1, N), borders(rng)))
def setup_inputs_border(rng):
    return make(rng, flags(rng, rng.integers(1, ST + 1, N), np.arange(N) == 0))
def setup_inputs_dense(rng):
    n = np.full(N, ST); n[0] = ST - rng.integers(1, N)
    return make(rng, flags(rng, n, borders(rng)))
def setup_inputs_one(rng):
    return make(rng, flags(rng, np.ones(N, int), np.arange(N) == 0))
def setup_inputs_spread(rng):
    return make(rng, flags(rng, rng.integers(1, ST + 1, N), borders(rng)), far=8, spread=True)
def setup_inputs_ties(rng):
    d = setup_inputs(rng)
    m = np.cumsum(flags(rng, rng.integers(1, ST + 1, N), borders(rng)).reshape(-1)) - 1; n = int(m[-1]) + 1
    u = np.zeros((128, 8, 4), np.float32); u[:64] = rng.choice([-1, 1], (64, 8, 4)) * rng.uniform(0.75, 1.25, (64, 8, 4))
    g = np.zeros((128, 1, 4), np.float32); g[64:] = rng.choice([-1, 1], (64, 1, 4))
    t = np.zeros((128, 128, 4), np.float32); t[:, :8] = u + g; t[:, 8:16] = u + g
    k = np.cumsum(rng.integers(1, 8, n)) % 8
    big = int(np.argmax(np.bincount(m)))
    k = (k - k[big]) % 8
    neg = rng.permutation(n) % 2
    c = u[:, k[m]] + g * np.where(neg[m] > 0, -2, 1).astype(np.float32)[:, None] + rng.standard_normal((128, N * T, 4), dtype=np.float32) * np.float32(0.125)
    c = c * np.exp2(rng.integers(-2, 3, (N * T, 1))).astype(np.float32)
    zero = (k[m] == 0) & (rng.random(N * T) < 0.25); zero[np.flatnonzero(m == big)[1]] = True
    c[:, zero] = 0
    d["x"] = mx_ref.flush(np.ascontiguousarray(c.reshape(128, N, 4 * T).transpose(1, 0, 2)).astype(BF))
    d["p"] = np.stack([mx_ref.flush(t.reshape(128, 512).astype(BF))] * N)
    return d
def labels(x, p):
    return np.stack([np.argmax(mx_ref.matmul(mx_ref.quantize(p[r]), mx_ref.quantize(x[r]))[:16] + np.float32(0.0), axis=0) for r in range(N)])
def starts(l):
    e = l.reshape(-1)
    return np.concatenate([[True], e[1:] != e[:-1]])
def check_inputs(d):
    b = []
    for r in range(N):
        if not np.array_equal(d["p"][r], d["p"][0]): b.append("p (the same on all ranks)")
        if d["p"][r][:, 64:].astype(np.float32).any(): b.append("p (zero columns)")
    n = starts(labels(d["x"], d["p"])).reshape(N, T).sum(axis=1)
    if n.min() < 1 or n.max() > ST: b.append("x (runs that start on a rank)")
    return b
def reference(x, p, a, w, v):
    l = labels(x, p); s = starts(l)
    m = np.add.accumulate(s.astype(int)) - 1
    first = np.flatnonzero(s)
    seq = np.concatenate([x[r] for r in range(N)], axis=1)
    h = []
    for r in range(N):
        e = np.full(ST, -1); mine = first[r::N]; e[:len(mine)] = mine
        c = mx_ref.quantize(cols(seq, e))
        h.append(tile([np.maximum(mx_ref.matmul(mx_ref.quantize(np.ascontiguousarray(cut(a[r], i))), c), np.float32(0)) * np.float32(0.05) for i in range(4)]))
    h = np.concatenate(h, axis=1)
    y = np.zeros((N, 128, T), np.float32); lb = np.zeros((N, 2, T), np.float32)
    for r in range(N):
        k = m[r * T:r * T + T]
        hk = mx_ref.quantize(cols(h, (k % N) * ST + k // N))
        y[r] = mx_ref.matmul(mx_ref.quantize(w[r]), mx_ref.quantize(x[r])) + mx_ref.matmul(mx_ref.quantize(v[r]), hk)
        lb[r, 0] = l[r]; lb[r, 1] = k
    return {"y": y, "lb": lb}

@@ -1,0 +1,449 @@
+from concourse.bass import DstId, RemoteDMATransfer
+from concourse.mybir import dt, AluOpType, ActivationFunctionType
+
+ALU = AluOpType
+ACT = ActivationFunctionType
+N = 4
+G = 32
+GT = 4 * G
+GB = G + 2
+LAND = GT
+X0 = 16
+X1 = X0 + 512
+XB = 16
+BIG = 1e25
+DUMP = 130
+FW = 776
+CC = 272
+
+SCRATCH = {}
+for _dtype, _names in {
+    "bfloat16": "pb 64 pt 576 xb 2064 ab 2048 wb 512 vb 512 nn 256 cc 272 la 64 lr 64 msg 16 msgin 8 bn 16 bc 16 sx 512 hb 512",
+    "float32": "zb 136 sc 256 rs 136 xm 264 eq 64 one 64 cn 64 nk 32 xa 32 rw 32 sf 16 sm 16 bs 32 bx 24 cf 32 ct 32 be 64 br 64 pf 16 pg 16 l4 8 "
+               "row 32 tq 32 mb 32 kn 8 kn2 8 kc 4 kd 32 ji 128 jv 512 fw 776 fm 128 yj 16 col 8 u 32 t1 16 t2 16 in2 32 ut 32 gf 32 cm 32 gx 32 "
+               "bf 32 ix 32 hv 136 wx 512 yb 512 lb0 32 lb1 32",
+    "int32": "pi 12 vi 2 ci 2 wi 32 zi 32 bi 32 ki 32",
+    "uint16": "lg16 4 of16 32 off16 2 ls16 32 ix16 32",
+    "float8_e4m3fn_x4": "pq 144 xq 544 bq 144 aq 512 wq 128 vq 128 cq 224 hq 232",
+    "uint8": "pz 144 xz 544 bz 144 az 512 wz 128 vz 128 cz 224 hz 232",
+}.items():
+    _l = _names.split()
+    for _n, _w in zip(_l[::2], _l[1::2]):
+        SCRATCH[_n] = ("sbuf", [128, int(_w)], _dtype)
+for _n in ("pl0", "pl1", "pwx", "pa0", "pa1", "pa2", "pa3", "pv"):
+    SCRATCH[_n] = ("psum", [128, 512], "float32")
+SEMAPHORES = ["sv", "sa", "st", "sg", "lrecv", "rrecv", "bloc", "mrecv", "mloc", "crecv", "cloc", "hrecv", "hloc",
+              "dp", "dx0", "dx1", "dx2", "dx3", "da", "dw", "dv", "dl0", "dl1", "dy0", "dy1", "dy2"]
+
+
+def tracker(g, T):
+    queues = {"v": g.vector, "a": g.scalar, "t": g.tensor, "g": g, "s": g.sync}
+    know = {q: {} for q in queues}
+    count = {}
+    acc = {}
+    order = [0]
+
+    def wait(q, tok):
+        sem, n, snap = tok
+        if know[q].get(sem, 0) < n:
+            queues[q].wait_ge(T.sem[sem], n)
+            for k, v in snap.items():
+                if know[q].get(k, 0) < v:
+                    know[q][k] = v
+            know[q][sem] = max(n, know[q].get(sem, 0))
+
+    def settle(q, reads, writes):
+        deps = []
+        for buf, a, b in reads:
+            deps += [(o, tok) for (c, d, w, tok, o) in acc.get(buf, []) if w and a < d and c < b]
+        for buf, a, b in writes:
+            deps += [(o, tok) for (c, d, w, tok, o) in acc.get(buf, []) if a < d and c < b]
+        for o, tok in sorted(deps, key=lambda z: -z[0]):
+            wait(q, tok)
+
+    def note(tok, reads, writes):
+        order[0] += 1
+        for buf, a, b in reads:
+            acc.setdefault(buf, []).append((a, b, False, tok, order[0]))
+        for buf, a, b in writes:
+            acc.setdefault(buf, []).append((a, b, True, tok, order[0]))
+
+    def emit(q, call, reads, writes, sem=None, inc=1, chain=False):
+        settle(q, reads, [] if chain else writes)
+        sem = sem or "s" + q
+        call().then_inc(T.sem[sem], inc)
+        count[sem] = count.get(sem, 0) + inc
+        note((sem, count[sem], dict(know[q])), reads, writes)
+
+    def remote(call, reads, sem, n):
+        settle("g", reads, [])
+        call()
+        count[sem] = count.get(sem, 0) + n
+
+    def arrives(sem, n, writes):
+        count[sem] = count.get(sem, 0) + n
+        note((sem, n, {}), [], writes)
+
+    def finish():
+        for sem, n in count.items():
+            wait("g", (sem, n, {}))
+
+    return emit, remote, arrives, finish
+
+
+def rank_program(g, core, T, topo):
+    s = T.rank_of(core)
+    if s is None:
+        return
+    emit, remote, arrives, finish = tracker(g, T)
+
+    def A(name, a, b):
+        return T[name][:, a:b]
+
+    def ap(t):
+        return T[t[0]][:, t[1]:t[2]:t[3]] if len(t) > 3 else T[t[0]][:, t[1]:t[2]]
+
+    def span(t):
+        return (t[0], t[1], t[2])
+
+    def dma(q, sem, out, in_, reads, writes):
+        eng = g.sync if q == "s" else g.scalar
+        emit(q, lambda: eng.dma_start(out, in_), reads, writes, sem=sem, inc=16)
+
+    def tt(o, x, y, op):
+        emit("v", lambda: g.vector.tensor_tensor(ap(o), ap(x), ap(y), op), [span(x), span(y)], [span(o)])
+
+    def ts(o, x, s1, s2, op0, op1=None):
+        r = [span(x)] + [span(z) for z in (s1, s2) if isinstance(z, tuple)]
+        c1 = ap(s1) if isinstance(s1, tuple) else s1
+        c2 = ap(s2) if isinstance(s2, tuple) else s2
+        if op1 is None:
+            emit("v", lambda: g.vector.tensor_scalar(ap(o), ap(x), c1, None, op0), r, [span(o)])
+        else:
+            emit("v", lambda: g.vector.tensor_scalar(ap(o), ap(x), c1, c2, op0, op1), r, [span(o)])
+
+    def cp(o, x, q="v"):
+        if q == "v":
+            emit("v", lambda: g.vector.tensor_copy(ap(o), ap(x)), [span(x)], [span(o)])
+        else:
+            emit("a", lambda: g.scalar.activation(ap(o), ap(x), ACT.Copy), [span(x)], [span(o)])
+
+    def act(o, x, bias, scale=1.0):
+        r = [span(x)] + ([span(bias)] if isinstance(bias, tuple) else [])
+        b = ap(bias) if isinstance(bias, tuple) else bias
+        emit("a", lambda: g.scalar.activation(ap(o), ap(x), ACT.Identity, bias=b, scale=scale), r, [span(o)])
+
+    def total(o, x, n):
+        emit("a", lambda: g.scalar.activation(A("yj", 0, n), ap(x), ACT.Copy, accum_out=ap(o)), [span(x)], [("yj", 0, n), span(o)])
+
+    def fill(o, c):
+        emit("v", lambda: g.vector.memset(ap(o), c), [], [span(o)])
+
+    def tr(o, x):
+        emit("v", lambda: g.vector.transpose(ap(o), ap(x)), [span(x)], [span(o)])
+
+    def scan(o, d0, d1, init, op0, op1):
+        r = [span(d0), span(d1)] + ([span(init)] if isinstance(init, tuple) else [])
+        c = ap(init) if isinstance(init, tuple) else init
+        emit("v", lambda: g.vector.tensor_tensor_scan(ap(o), ap(d0), ap(d1), c, op0, op1), r, [span(o)])
+
+    def quant(cq, cz, a, src, b, n):
+        emit("v", lambda: g.vector.quantize_mx(A(cq, a, a + n), A(cz, a, a + n), A(src, 4 * b, 4 * b + 4 * n)),
+             [(src, 4 * b, 4 * b + 4 * n)], [(cq, a, a + n), (cz, a, a + n)])
+
+    def mm(o, lq, lz, a, rq, rz, b, n, start=True, stop=True):
+        emit("t", lambda: g.tensor.matmul_mx(A(o, 0, n), A(lq, a, a + 128), A(lz, a, a + 128), A(rq, b, b + n), A(rz, b, b + n), start, stop),
+             [(lq, a, a + 128), (lz, a, a + 128), (rq, b, b + n), (rz, b, b + n)], [(o, 0, 512)], chain=not start)
+
+    def iota(o, pattern, base, cm=0):
+        if o[0] == "pi":
+            emit("g", lambda: g.iota(ap(o), pattern, base, cm), [], [span(o)])
+        else:
+            emit("g", lambda: g.iota(ap(o), pattern, base, cm, allow_small_or_imprecise_dtypes=True), [], [span(o)])
+
+    def pick(q, o, win, off, a, b):
+        w = ap(win).indirect(T[off][:, a:b])
+        r = [span(win), (off, a, b)]
+        if q == "v":
+            emit("v", lambda: g.vector.tensor_copy(ap(o), w), r, [span(o)])
+        else:
+            emit("a", lambda: g.scalar.activation(ap(o), w, ACT.Copy), r, [span(o)])
+
+    def shared(src, dsts):
+        return [e for e in topo.engines(src, dsts[0]) if all(e in topo.engines(src, d) for d in dsts)]
+
+    def mask(engines):
+        return sum(1 << e for e in engines)
+
+    def where(d):
+        rid, pid, _ = topo.addr(d)
+        return DstId(rid=rid, pnc=pid)
+
+    dma("a", "dp", A("pb", 0, 64), T.p[:, 0:64], [], [("pb", 0, 64)])
+    for k, que in enumerate("sasa"):
+        c = XB + 512 * k
+        dma(que, "dx%d" % k, A("xb", c, c + 512), T.x[:, 512 * k:512 * k + 512], [], [("xb", c, c + 512)])
+    dma("s", "da", A("ab", 0, 2048), T.a[:, 0:2048], [], [("ab", 0, 2048)])
+
+    iota(("pi", 0, 2), [[-15, 2]], 15, 1)
+    iota(("row", 0, 16), [[1, 16]], 0)
+    iota(("tq", 0, 32), [[0, 8], [1, 4]], 0)
+    iota(("kc", 0, 4), [[32, 4]], 0)
+    iota(("ji", 0, 128), [[4, 8], [128, 16]], 0)
+    iota(("kd", 0, 32), [[-1, 32]], DUMP + 511)
+    iota(("kn", 0, 2), [[2, 2]], s - 6)
+    fill(("zb", 0, 136), 0.0)
+    fill(("pt", 0, 576), 0.0)
+    cp(("xb", 0, XB), ("zb", 0, XB), "a")
+    act(("rs", 0, 136), ("zb", 0, 136), BIG)
+    for o, c in ((2, 15), (4, 3)):
+        ts(("pi", o, o + 2), ("pi", 0, 2), c, None, ALU.bitwise_and)
+    for o, c, d in ((6, 2, 3), (8, 3, 1), (10, 4, 1)):
+        ts(("pi", o, o + 2), ("pi", 0, 2), c, d, ALU.logical_shift_right, ALU.bitwise_and)
+    for k in range(4):
+        cp(("pt", 64 + 128 * k, 128 + 128 * k), ("pb", 0, 64), "va"[k // 2])
+    act(("rs", 0, 136, 16), ("zb", 0, 9), -BIG)
+    act(("xm", 0, 1), ("zb", 0, 1), -BIG)
+    act(("bx", 0, 1), ("zb", 0, 1), -BIG)
+    quant("pq", "pz", 0, "pt", 0, 144)
+
+    def border(d, a, za, bq, b, bz, zb, rsem):
+        e = shared(core, [d])
+        h = len(e) // 2
+        moves = [RemoteDMATransfer(dst_ids=[where(d)], dma_engine_mask=mask(e[:h]), remote_sem=T.sem[rsem],
+                                   srcs=[A("xq", a, a + 2).bitcast(dt.uint8)], dsts=[A(bq, b, b + 2).bitcast(dt.uint8)]),
+                 RemoteDMATransfer(dst_ids=[where(d)], dma_engine_mask=mask(e[h:]), remote_sem=T.sem[rsem],
+                                   srcs=[A("xz", za, za + 8)], dsts=[A(bz, zb, zb + 8)])]
+        remote(lambda: g.remote_dma_fused(moves, local_sem=T.sem.bloc), [("xq", a, a + 2), ("xz", za, za + 8)], "bloc", len(e))
+
+    def argmax(pl, c, n, bufs):
+        sc, xm, nn_, cc, o, w = bufs
+        return [lambda: tr((sc, o, o + n), (pl, c, c + n)),
+                lambda: scan((xm, o + 1, o + w + 1), (sc, o, o + w), ("rs", 1, w + 1), -BIG, ALU.max, ALU.min),
+                lambda: tt((nn_, o, o + w), (sc, o, o + w), (xm, o, o + w), ALU.is_le),
+                lambda: scan((cc, o, o + w), (nn_, o, o + w), (nn_, o, o + w), 0.0, ALU.mult, ALU.add)]
+
+    def quarter(c):
+        n = 2 if c == 0 and s else 0
+        quant("xq", "xz", X0 + 128 * c - n, "xb", XB // 4 + 128 * c - n, 128 + n)
+
+    def score(c):
+        mm("pl%d" % (c // 2), "pq", "pz", 16 - 16 * (c % 2), "xq", "xz", X0 + 128 * c, 128, c % 2 == 0, c % 2 == 1)
+
+    edge = ("bs", "bx", "bn", "bc", 0, 16)
+    half0 = argmax("pl0", 0, 128, ("sc", "xm", "nn", "cc", 0, 128))
+    half1 = argmax("pl1", 0, 128, ("sc", "xm", "nn", "cc", 128, 128))
+    right = argmax("pwx", 96, 32, edge) if s < N - 1 else [lambda: None] * 4
+
+    quarter(0)
+    if s:
+        border(T.cores[s - 1], X0 - 1, X0 - 1, "xq", X1, "xz", X1, "rrecv")
+    if s < N - 1:
+        arrives("rrecv", len(shared(T.cores[s + 1], [core])), [("xq", X1, X1 + 2), ("xz", X1, X1 + 8)])
+    score(0)
+    cp(("pf", 0, 10), ("pi", 2, 12))
+    p16, p4, pd4, pd8, pd16 = [("pf", k, k + 1) for k in (1, 3, 5, 7, 9)]
+    pg = [("pg", k, k + 1) for k in range(16)]
+    quarter(1)
+    score(1)
+    act(("one", 0, 64), ("zb", 0, 64), 1.0)
+    act(("eq", 32, 64), ("zb", 0, 32), 1.0)
+    act(("cc", 256, CC), ("zb", 0, CC - 256), -1.0)
+    for k in range(2):
+        act(pg[2 + k], ("pf", 2 + k, 3 + k), 15.0, 32.0)
+    for k in range(2):
+        act(pg[4 + k], ("pf", 4 + k, 5 + k), pg[2 + k], 16.0)
+    for k in range(2):
+        act(pg[6 + k], ("pf", 6 + k, 7 + k), pg[4 + k], 96.0)
+    act(pg[0], pd16, 1.0, -1.0)
+    act(pg[1], pd4, 3.0, -1.0)
+    act(("l4", 2, 4), ("zb", 0, 2), pg[7])
+    act(pg[9], p16, 0.0, -32.0)
+    act(pg[10], p16, 31.0, -4.0)
+    act(pg[11], pd8, pg[10], 32.0)
+    act(("kd", 0, 32), ("kd", 0, 32), pg[9])
+    act(("kc", 0, 4), ("kc", 0, 4), p4)
+    act(("kn", 0, 2), ("kn", 0, 2), pd8)
+    for k in range(4):
+        act(("jv", 128 * k, 128 * k + 128), ("ji", 0, 128), ("kc", k, k + 1))
+    act(("fw", 0, 128), ("ji", 0, 128), p4, 0.0)
+    ts(pg[8], p16, 0.0, 1.0, ALU.is_equal, ALU.mult)
+    half0[0]()
+    ts(("sm", 0, 16), ("row", 0, 16), p16, None, ALU.not_equal)
+    half0[1]()
+    quarter(2)
+    score(2)
+    quarter(3)
+    if s < N - 1:
+        border(T.cores[s + 1], X1 - 2, X1 - 8, "bq", 14, "bz", 8, "lrecv")
+    if s:
+        arrives("lrecv", len(shared(T.cores[s - 1], [core])), [("bq", 14, 16), ("bz", 8, 16)])
+    score(3)
+    if s < N - 1:
+        mm("pwx", "pq", "pz", 16, "xq", "xz", X1 + 2 - 128, 128)
+    half0[2]()
+    ts(("l4", 0, 2), ("zb", 0, 2), pg[6], pg[8], ALU.add, ALU.add)
+    half0[3]()
+    half1[0]()
+    ts(("mb", 0, 32), ("tq", 0, 32), pg[1], -BIG, ALU.is_equal, ALU.mult)
+    half1[1]()
+    cp(("lg16", 0, 4), ("l4", 0, 4))
+    half1[2]()
+    half1[3]()
+
+    pick("v", ("la", 0, 64), ("cc", 0, CC), "lg16", 0, 4)
+    right[0]()
+    tr(("lr", 0, 64), ("la", 0, 64))
+    right[1]()
+    tt(("eq", 0, 32), ("lr", 32, 64), ("lr", 31, 63), ALU.is_equal)
+    right[2]()
+    scan(("cn", 0, 64), ("eq", 0, 64), ("one", 0, 64), 0.0, ALU.add, ALU.subtract)
+    right[3]()
+    tt(("nk", 0, 32), ("eq", 0, 32), ("kd", 0, 32), ALU.mult)
+    tr(("rw", 0, 32), ("cn", 32, 64))
+    if s < N - 1:
+        ts(("cf", 0, 32), ("zb", 0, 32), ("bc", 15, 16), ("lr", 63, 64), ALU.add, ALU.is_equal)
+    tt(("xa", 0, 32), ("nk", 0, 32), ("cn", 0, 32), ALU.add)
+    scan(("sf", 0, 16), ("sm", 0, 16), ("rw", 0, 16), 0.0, ALU.mult, ALU.add)
+    if s < N - 1:
+        tr(("ct", 0, 32), ("cf", 0, 32))
+    own = ("sf", 15, 16)
+    nn = ("col", 2, 3)
+    total(nn, ("rw", 0, 16), 16)
+    ts(("of16", 0, 32), ("xa", 0, 32), own, None, ALU.subtract)
+    later = [T.cores[d] for d in range(s + 1, N)]
+    if later:
+        scan(("msg", 0, 16), ("rw", 0, 16), ("zb", 0, 16), ("ct", 31, 32), ALU.add, ALU.add)
+        eng = shared(core, later)
+        remote(lambda: g.remote_dma_fused([RemoteDMATransfer(dst_ids=[where(d) for d in later], dma_engine_mask=mask(eng), remote_sem=T.sem.mrecv,
+                                                             srcs=[A("msg", 15, 16)], dsts=[A("msgin", s, s + 1) for _ in later])],
+                                          local_sem=T.sem.mloc), [("msg", 15, 16)], "mloc", len(eng))
+    if s:
+        arrives("mrecv", sum(len(shared(T.cores[r], [T.cores[d] for d in range(r + 1, N)])) for r in range(s)), [("msgin", 0, s)])
+    dma("s", "dw", A("wb", 0, 512), T.w[:, 0:512], [("msg", 15, 16), ("of16", 0, 32)], [("wb", 0, 512)])
+    dma("s", "dv", A("vb", 0, 512), T.v[:, 0:512], [], [("vb", 0, 512)])
+    act(("kn2", 0, 2), ("kn", 0, 2), nn)
+    emit("v", lambda: g.vector.tensor_copy(T.fw[:, 0:FW].indirect(T.of16[:, 0:32]), A("jv", 0, 512)),
+         [("jv", 0, 512), ("of16", 0, 32)], [("fw", 0, FW)])
+
+    Y = ("msgin", 0, 1)
+    if s > 1:
+        Y = ("col", 0, 1)
+        total(Y, ("msgin", 0, s), s)
+
+    def wrap(k):
+        scan(("fm", 32 * k, 32 * k + 32), ("mb", 0, 32), ("fw", k, 128, 4), 0.0, ALU.add, ALU.max)
+
+    if s:
+        ts(("vi", 0, 2), ("kn2", 0, 2), Y, -1.0, ALU.add, ALU.mult)
+    else:
+        ts(("vi", 0, 2), ("kn2", 0, 2), -1.0, None, ALU.mult)
+    wrap(0)
+    wrap(1)
+    ts(("ci", 0, 2), ("vi", 0, 2), 3, None, ALU.bitwise_and)
+    wrap(2)
+    wrap(3)
+    ts(("off16", 0, 2), ("ci", 0, 2), 32.0, pg[11], ALU.mult, ALU.add)
+    pick("v", ("ls16", 0, 32), ("fm", 0, 128), "off16", 0, 2)
+    pick("a", ("sx", 288, 4 * GT), ("xb", XB, XB + 2048), "ls16", 18, 32)
+    pick("v", ("sx", 0, 288), ("xb", XB, XB + 2048), "ls16", 0, 18)
+    quant("cq", "cz", 0, "sx", 0, GT)
+
+    peers = [T.cores[(s + i) % N] for i in (1, 2, 3)]
+    eng = shared(core, peers)
+    q = len(eng) // 4
+    code_eng = [eng[0:2 * q], eng[2 * q:3 * q], eng[3 * q:4 * q]]
+    scale_eng = [eng[0:q], eng[q:2 * q], eng[2 * q:4 * q]]
+
+    def hop(cq, cz, width, src, land, rsem, lsem):
+        for codes in (True, False):
+            moves = []
+            for i in (1, 2, 3):
+                a, b = src(i), land(i)
+                if codes:
+                    x, y = A(cq, a, a + width).bitcast(dt.uint8), A(cq, b, b + width).bitcast(dt.uint8)
+                else:
+                    x, y = A(cz, a, a + width), A(cz, b, b + width)
+                moves.append(RemoteDMATransfer(dst_ids=[where(peers[i - 1])], dma_engine_mask=mask((code_eng if codes else scale_eng)[i - 1]),
+                                               remote_sem=T.sem[rsem], srcs=[x], dsts=[y]))
+            lo, hi = src(1), src(3) + width
+            remote(lambda: g.remote_dma_fused(moves, local_sem=T.sem[lsem]), [(cq, lo, hi), (cz, lo, hi)], lsem, 4 * q)
+
+    hop("cq", "cz", G, lambda i: G * (i - 1), lambda i: LAND + G * (3 - i), "crecv", "cloc")
+    arrives("crecv", 8 * q, [("cq", LAND, LAND + 3 * G), ("cz", LAND, LAND + 3 * G)])
+
+    left = [lambda: None] * 4
+    if s:
+        quant("bq", "bz", 16, "xb", XB // 4, 128)
+        mm("pl1", "pq", "pz", 16, "bq", "bz", 14, 128)
+        left = argmax("pl1", 0, 32, edge)
+        act(("be", 32, 64), ("zb", 0, 32), ("lr", 32, 33))
+    act(("lb0", 0, 32), ("lr", 32, 64), 15.0, -1.0)
+    quant("aq", "az", 0, "ab", 0, 512)
+    left[0]()
+    quant("wq", "wz", 0, "wb", 0, 128)
+    mm("pwx", "wq", "wz", 0, "xq", "xz", X0, 512)
+    left[1]()
+    quant("vq", "vz", 0, "vb", 0, 128)
+    left[2]()
+    nE = ("col", 1, 2)
+    ts(("u", 0, 32), ("cn", 0, 32), own, None, ALU.subtract)
+    if s:
+        ts(nE, nn, Y, 1.0, ALU.add, ALU.add)
+    else:
+        ts(nE, nn, 1.0, None, ALU.add)
+    left[3]()
+    if s:
+        act(("be", 0, 32), ("zb", 0, 32), ("bc", 15, 16))
+    cp(("wx", 0, 512), ("pwx", 0, 512), "a")
+    ts(("t1", 0, 16), ("u", 0, 16), pg[0], None, ALU.mult)
+    ts(("t2", 0, 16), ("u", 16, 32), pd16, None, ALU.mult)
+    ts(("lb1", 0, 32), ("u", 0, 32), nE, -1.0, ALU.add, ALU.mult)
+    tt(("in2", 0, 16), ("t1", 0, 16), ("t2", 0, 16), ALU.add)
+    tt(("in2", 16, 32), ("t1", 0, 16), ("t2", 0, 16), ALU.add)
+    if s:
+        tr(("br", 0, 64), ("be", 0, 64))
+    tr(("ut", 0, 32), ("in2", 0, 32))
+    dma("s", "dl0", T.lb[0:1, :], T.lb0[0:16, :], [("lb0", 0, 32)], [])
+    dma("s", "dl1", T.lb[1:2, :], T.lb1[0:16, :], [("lb1", 0, 32)], [])
+
+    for i in range(4):
+        mm("pa%d" % i, "aq", "az", 128 * i, "cq", "cz", 3 * G, GT)
+    for i in range(4):
+        o = ("hb", i, 4 * GT, 4)
+        r, w = [("pa%d" % i, 0, 512)], [("hb", i * 4 * GT, i * 4 * GT + 1)]
+        if i % 2 == 0:
+            emit("a", lambda: g.scalar.activation(ap(o), A("pa%d" % i, 0, GT), ACT.Relu, scale=0.05), r, w)
+        else:
+            emit("v", lambda: g.vector.tensor_scalar(ap(o), A("pa%d" % i, 0, GT), 0.0, 0.05, ALU.max, ALU.mult), r, w)
+    emit("v", lambda: g.vector.quantize_mx(A("hq", 0, GT), A("hz", 0, GT), A("hb", 0, 4 * GT)), [("hb", 0, 16 * GT)], [("hq", 0, GT), ("hz", 0, GT)])
+    hop("hq", "hz", GB, lambda i: G * i - 2, lambda i: LAND + GB * (i - 1), "hrecv", "hloc")
+    arrives("hrecv", 8 * q, [("hq", LAND, LAND + 3 * GB), ("hz", LAND, LAND + 3 * GB)])
+
+    mm("pv", "vq", "vz", 0, "hq", "hz", 0, GT)
+    cp(("hv", 2, GB), ("pv", 0, G), "a")
+    cp(("hv", 0, 2), ("pv", GT - 2, GT), "a")
+    for d in range(2):
+        emit("v", lambda: g.vector.tensor_copy(T.wi[:, d:32:2], A("ut", 16 * d, 16 * d + 16)), [("ut", 0, 32)], [("wi", 16 * d, 16 * d + 16)])
+    ts(("ki", 0, 32), ("wi", 0, 32), 2, None, ALU.logical_shift_right)
+    ts(("zi", 0, 32), ("wi", 0, 32), nE, float(s + 1024), ALU.add, ALU.add)
+    if s:
+        ts(("cm", 0, 32), ("wi", 0, 32), nn, -1.0, ALU.add, ALU.is_equal)
+        ts(("col", 3, 4), ("br", 1, 2), ("br", 32, 33), -1.0, ALU.is_equal, ALU.mult)
+    ts(("gf", 0, 32), ("ki", 0, 32), -1.0, float(G), ALU.mult, ALU.add)
+    ts(("bi", 0, 32), ("zi", 0, 32), 3, None, ALU.bitwise_and)
+    if s:
+        ts(("cm", 0, 32), ("cm", 0, 32), ("col", 3, 4), 1.0, ALU.mult, ALU.add)
+    ts(("bf", 0, 32), ("bi", 0, 32), float(GB), 1.0, ALU.mult, ALU.add)
+    if s:
+        tt(("gx", 0, 32), ("gf", 0, 32), ("cm", 0, 32), ALU.mult)
+    tt(("ix", 0, 32), ("gx" if s else "gf", 0, 32), ("bf", 0, 32), ALU.add)
+    cp(("ix16", 0, 32), ("ix", 0, 32))
+
+    mm("pl0", "vq", "vz", 0, "hq", "hz", LAND + 3 * GB - 128, 128)
+    cp(("hv", GB, 4 * GB), ("pl0", 128 - 3 * GB, 128))
+    for k, (c, d) in enumerate(((0, 160), (160, 352), (352, 512))):
+        emit("v", lambda: g.vector.tensor_tensor(A("yb", c, d), T.hv[:, 0:4 * GB].indirect(T.ix16[:, c // 16:d // 16]), A("wx", c, d), ALU.add),
+             [("hv", 0, 4 * GB), ("ix16", 0, 32), ("wx", c, d)], [("yb", c, d)])
+        dma("sas"[k], "dy%d" % k, T.y[:, c:d], A("yb", c, d), [("yb", c, d)], [])
+    finish()

@@ -7,33 +7,37 @@ N = 4
 G = 32
 GT = 4 * G
 GB = G + 2
-LAND = GT
+CL = 2 * GT
+HL = 3 * GT
+SX = 16 + 2048
 X0 = 16
 X1 = X0 + 512
 XB = 16
 BIG = 1e25
-DUMP = 130
-FW = 776
+W0 = 32
+FW = 800
+TAB = 528
 CC = 272
+STAGES = ((1, 2, 3),)
 
 SCRATCH = {}
 for _dtype, _names in {
-    "bfloat16": "pb 64 pt 576 xb 2064 ab 2048 wb 512 vb 512 nn 256 cc 272 la 64 lr 64 msg 16 msgin 8 bn 16 bc 16 sx 512 hb 512",
-    "float32": "zb 136 sc 256 rs 136 xm 264 eq 64 one 64 cn 64 nk 32 xa 32 rw 32 sf 16 sm 16 bs 32 bx 24 cf 32 ct 32 be 64 br 64 pf 16 pg 16 l4 8 "
-               "row 32 tq 32 mb 32 kn 8 kn2 8 kc 4 kd 32 ji 128 jv 512 fw 776 fm 128 yj 16 col 8 u 32 t1 16 t2 16 in2 32 ut 32 gf 32 cm 32 gx 32 "
+    "bfloat16": "pb 64 pt 576 xb 2576 ab 2048 wb 512 vb 512 nn 256 cc 272 la 64 lr 64 msg 16 msgin 8 bn 16 bc 16 hb 768 tab 528 sl 8 eb 512",
+    "float32": "zb 136 sc 256 rs 136 xm 264 eq 96 one 96 cn 96 nk 32 xa 32 rw 64 sf 16 sm 16 bs 32 bx 24 be 64 br 64 pf 16 pg 16 l4 16 "
+               "row 32 kn 8 kn2 8 kd 32 ji 128 jv 256 fw 800 ft 128 fa 64 fb 32 fm 32 yj 16 col 8 u 32 t1 16 t2 16 in2 32 ut 32 gf 32 cm 32 gx 32 "
                "bf 32 ix 32 hv 136 wx 512 yb 512 lb0 32 lb1 32",
-    "int32": "pi 12 vi 2 ci 2 wi 32 zi 32 bi 32 ki 32",
-    "uint16": "lg16 4 of16 32 off16 2 ls16 32 ix16 32",
-    "float8_e4m3fn_x4": "pq 144 xq 544 bq 144 aq 512 wq 128 vq 128 cq 224 hq 232",
-    "uint8": "pz 144 xz 544 bz 144 az 512 wz 128 vz 128 cz 224 hz 232",
+    "int32": "pi 12 wi 32 wv 32 zi 32 bi 32 ki 32 kj 32",
+    "uint16": "lg16 16 of16 16 zi16 2 off16 16 ls16 64 ix16 32",
+    "float8_e4m3fn_x4": "pq 144 xq 544 bq 144 aq 512 wq 128 vq 128 cq 352 hq 488 nq 128",
+    "uint8": "pz 144 xz 544 bz 144 az 512 wz 128 vz 128 cz 352 hz 488 nz 128",
 }.items():
     _l = _names.split()
     for _n, _w in zip(_l[::2], _l[1::2]):
         SCRATCH[_n] = ("sbuf", [128, int(_w)], _dtype)
 for _n in ("pl0", "pl1", "pwx", "pa0", "pa1", "pa2", "pa3", "pv"):
     SCRATCH[_n] = ("psum", [128, 512], "float32")
-SEMAPHORES = ["sv", "sa", "st", "sg", "lrecv", "rrecv", "bloc", "mrecv", "mloc", "crecv", "cloc", "hrecv", "hloc",
-              "dp", "dx0", "dx1", "dx2", "dx3", "da", "dw", "dv", "dl0", "dl1", "dy0", "dy1", "dy2"]
+SEMAPHORES = ["sv", "sa", "st", "sg", "lrecv", "rrecv", "bnq", "bxq", "mrecv", "mloc", "crecv0", "crecv1", "crecv2", "cloc", "hrecv0", "hrecv1", "hrecv2", "hloc",
+              "dp", "de", "dx0", "dx1", "dx2", "dx3", "da", "dw", "dv", "dl0", "dl1", "dy0", "dy1", "dy2"]
 
 
 def tracker(g, T):
@@ -128,10 +132,10 @@ def rank_program(g, core, T, topo):
         else:
             emit("a", lambda: g.scalar.activation(ap(o), ap(x), ACT.Copy), [span(x)], [span(o)])
 
-    def act(o, x, bias, scale=1.0):
+    def act(o, x, bias, scale=1.0, f=ACT.Identity):
         r = [span(x)] + ([span(bias)] if isinstance(bias, tuple) else [])
         b = ap(bias) if isinstance(bias, tuple) else bias
-        emit("a", lambda: g.scalar.activation(ap(o), ap(x), ACT.Identity, bias=b, scale=scale), r, [span(o)])
+        emit("a", lambda: g.scalar.activation(ap(o), ap(x), f, bias=b, scale=scale), r, [span(o)])
 
     def total(o, x, n):
         emit("a", lambda: g.scalar.activation(A("yj", 0, n), ap(x), ACT.Copy, accum_out=ap(o)), [span(x)], [("yj", 0, n), span(o)])
@@ -161,10 +165,12 @@ def rank_program(g, core, T, topo):
         else:
             emit("g", lambda: g.iota(ap(o), pattern, base, cm, allow_small_or_imprecise_dtypes=True), [], [span(o)])
 
-    def pick(q, o, win, off, a, b):
+    def pick(q, o, win, off, a, b, plus=None, c=0.0):
         w = ap(win).indirect(T[off][:, a:b])
         r = [span(win), (off, a, b)]
-        if q == "v":
+        if plus:
+            emit("v", lambda: g.vector.tensor_scalar(ap(o), w, ap(plus), c, ALU.add, ALU.add), r + [span(plus)], [span(o)])
+        elif q == "v":
             emit("v", lambda: g.vector.tensor_copy(ap(o), w), r, [span(o)])
         else:
             emit("a", lambda: g.scalar.activation(ap(o), w, ACT.Copy), r, [span(o)])
@@ -180,6 +186,7 @@ def rank_program(g, core, T, topo):
         return DstId(rid=rid, pnc=pid)
 
     dma("a", "dp", A("pb", 0, 64), T.p[:, 0:64], [], [("pb", 0, 64)])
+    dma("s", "de", A("eb", 24, 32), T.x[:, 0:8] if s else T.x[:, 2040:2048], [], [("eb", 24, 32)])
     for k, que in enumerate("sasa"):
         c = XB + 512 * k
         dma(que, "dx%d" % k, A("xb", c, c + 512), T.x[:, 512 * k:512 * k + 512], [], [("xb", c, c + 512)])
@@ -187,34 +194,42 @@ def rank_program(g, core, T, topo):
 
     iota(("pi", 0, 2), [[-15, 2]], 15, 1)
     iota(("row", 0, 16), [[1, 16]], 0)
-    iota(("tq", 0, 32), [[0, 8], [1, 4]], 0)
-    iota(("kc", 0, 4), [[32, 4]], 0)
     iota(("ji", 0, 128), [[4, 8], [128, 16]], 0)
-    iota(("kd", 0, 32), [[-1, 32]], DUMP + 511)
-    iota(("kn", 0, 2), [[2, 2]], s - 6)
+    iota(("kd", 0, 32), [[1, 32]], 129)
     fill(("zb", 0, 136), 0.0)
+    fill(("eb", 0, 24), 0.0)
+    fill(("eb", 32, 512), 0.0)
     fill(("pt", 0, 576), 0.0)
-    cp(("xb", 0, XB), ("zb", 0, XB), "a")
+    if len(STAGES) > 1:
+        emit("v", lambda: g.vector.memset(A("hb", 0, 8 * G), 0.0), [], [("hb", 0, 1)])
     act(("rs", 0, 136), ("zb", 0, 136), BIG)
     for o, c in ((2, 15), (4, 3)):
         ts(("pi", o, o + 2), ("pi", 0, 2), c, None, ALU.bitwise_and)
     for o, c, d in ((6, 2, 3), (8, 3, 1), (10, 4, 1)):
         ts(("pi", o, o + 2), ("pi", 0, 2), c, d, ALU.logical_shift_right, ALU.bitwise_and)
+
+    def border(d, xq, a, xz, za, bq, b, bz, zb, rsem):
+        e = shared(core, [d])
+        h = len(e) // 2
+        moves = [RemoteDMATransfer(dst_ids=[where(d)], dma_engine_mask=mask(e[:h]), remote_sem=T.sem[rsem],
+                                   srcs=[A(xq, a, a + 2).bitcast(dt.uint8)], dsts=[A(bq, b, b + 2).bitcast(dt.uint8)]),
+                 RemoteDMATransfer(dst_ids=[where(d)], dma_engine_mask=mask(e[h:]), remote_sem=T.sem[rsem],
+                                   srcs=[A(xz, za, za + 8)], dsts=[A(bz, zb, zb + 8)])]
+        remote(lambda: g.remote_dma_fused(moves, local_sem=T.sem["b" + xq]), [(xq, a, a + 2), (xz, za, za + 8)], "b" + xq, len(e))
+        return len(e)
+
+    quant("nq", "nz", 0, "eb", 0, 128)
+    if s:
+        n = border(T.cores[s - 1], "nq", 5, "nz", 5, "xq", X1, "xz", X1, "rrecv")
+    else:
+        n = border(T.cores[1], "nq", 6, "nz", 0, "bq", 14, "bz", 8, "lrecv")
+    iota(("tab", 0, TAB), [[0, TAB // 4], [-1, 4]], 3)
     for k in range(4):
         cp(("pt", 64 + 128 * k, 128 + 128 * k), ("pb", 0, 64), "va"[k // 2])
     act(("rs", 0, 136, 16), ("zb", 0, 9), -BIG)
     act(("xm", 0, 1), ("zb", 0, 1), -BIG)
     act(("bx", 0, 1), ("zb", 0, 1), -BIG)
     quant("pq", "pz", 0, "pt", 0, 144)
-
-    def border(d, a, za, bq, b, bz, zb, rsem):
-        e = shared(core, [d])
-        h = len(e) // 2
-        moves = [RemoteDMATransfer(dst_ids=[where(d)], dma_engine_mask=mask(e[:h]), remote_sem=T.sem[rsem],
-                                   srcs=[A("xq", a, a + 2).bitcast(dt.uint8)], dsts=[A(bq, b, b + 2).bitcast(dt.uint8)]),
-                 RemoteDMATransfer(dst_ids=[where(d)], dma_engine_mask=mask(e[h:]), remote_sem=T.sem[rsem],
-                                   srcs=[A("xz", za, za + 8)], dsts=[A(bz, zb, zb + 8)])]
-        remote(lambda: g.remote_dma_fused(moves, local_sem=T.sem.bloc), [("xq", a, a + 2), ("xz", za, za + 8)], "bloc", len(e))
 
     def argmax(pl, c, n, bufs):
         sc, xm, nn_, cc, o, w = bufs
@@ -224,8 +239,7 @@ def rank_program(g, core, T, topo):
                 lambda: scan((cc, o, o + w), (nn_, o, o + w), (nn_, o, o + w), 0.0, ALU.mult, ALU.add)]
 
     def quarter(c):
-        n = 2 if c == 0 and s else 0
-        quant("xq", "xz", X0 + 128 * c - n, "xb", XB // 4 + 128 * c - n, 128 + n)
+        quant("xq", "xz", X0 + 128 * c, "xb", XB // 4 + 128 * c, 128)
 
     def score(c):
         mm("pl%d" % (c // 2), "pq", "pz", 16 - 16 * (c % 2), "xq", "xz", X0 + 128 * c, 128, c % 2 == 0, c % 2 == 1)
@@ -236,142 +250,190 @@ def rank_program(g, core, T, topo):
     right = argmax("pwx", 96, 32, edge) if s < N - 1 else [lambda: None] * 4
 
     quarter(0)
-    if s:
-        border(T.cores[s - 1], X0 - 1, X0 - 1, "xq", X1, "xz", X1, "rrecv")
     if s < N - 1:
         arrives("rrecv", len(shared(T.cores[s + 1], [core])), [("xq", X1, X1 + 2), ("xz", X1, X1 + 8)])
     score(0)
+    quarter(1)
+    score(1)
     cp(("pf", 0, 10), ("pi", 2, 12))
     p16, p4, pd4, pd8, pd16 = [("pf", k, k + 1) for k in (1, 3, 5, 7, 9)]
     pg = [("pg", k, k + 1) for k in range(16)]
-    quarter(1)
-    score(1)
-    act(("one", 0, 64), ("zb", 0, 64), 1.0)
-    act(("eq", 32, 64), ("zb", 0, 32), 1.0)
     act(("cc", 256, CC), ("zb", 0, CC - 256), -1.0)
-    for k in range(2):
-        act(pg[2 + k], ("pf", 2 + k, 3 + k), 15.0, 32.0)
-    for k in range(2):
-        act(pg[4 + k], ("pf", 4 + k, 5 + k), pg[2 + k], 16.0)
-    for k in range(2):
-        act(pg[6 + k], ("pf", 6 + k, 7 + k), pg[4 + k], 96.0)
-    act(pg[0], pd16, 1.0, -1.0)
-    act(pg[1], pd4, 3.0, -1.0)
+    act(("one", 0, 96), ("zb", 0, 96), 1.0)
+    act(("eq", 32, 96), ("zb", 0, 64), 1.0)
+    act(pg[8], p16, 1.0, -1.0, ACT.Relu)
+    act(pg[3], ("pf", 3, 4), 15.0, 32.0)
+    act(pg[8], pg[8], 15.0)
+    act(pg[5], ("pf", 5, 6), pg[3], 16.0)
+    act(pg[2], ("pf", 2, 3), pg[8], 32.0)
+    act(pg[7], ("pf", 7, 8), pg[5], 96.0)
+    act(pg[4], ("pf", 4, 5), pg[2], 16.0)
     act(("l4", 2, 4), ("zb", 0, 2), pg[7])
-    act(pg[9], p16, 0.0, -32.0)
-    act(pg[10], p16, 31.0, -4.0)
-    act(pg[11], pd8, pg[10], 32.0)
+    act(pg[6], ("pf", 6, 7), pg[4], 96.0)
+    act(pg[1], pd16, p16, 16.0)
+    act(("l4", 0, 2), ("zb", 0, 2), pg[6])
+    act(pg[9], p16, 0.0, 32.0)
+    act(("l4", 4, 6), ("zb", 0, 2), pg[1])
+    act(("sl", 0, 1), p16, 15.0, -1.0, ACT.Sign)
     act(("kd", 0, 32), ("kd", 0, 32), pg[9])
-    act(("kc", 0, 4), ("kc", 0, 4), p4)
-    act(("kn", 0, 2), ("kn", 0, 2), pd8)
-    for k in range(4):
-        act(("jv", 128 * k, 128 * k + 128), ("ji", 0, 128), ("kc", k, k + 1))
-    act(("fw", 0, 128), ("ji", 0, 128), p4, 0.0)
-    ts(pg[8], p16, 0.0, 1.0, ALU.is_equal, ALU.mult)
-    half0[0]()
-    ts(("sm", 0, 16), ("row", 0, 16), p16, None, ALU.not_equal)
-    half0[1]()
+    act(("sm", 0, 16), ("row", 0, 16), p16, -1.0, ACT.Sign)
+    act(pg[14], pd16, 0.0, 64.0)
+    act(("sm", 0, 16), ("sm", 0, 16), 0.0, 1.0, ACT.Abs)
+    act(pg[15], pd16, 32.0, 64.0)
+    act(("fw", W0, W0 + 128), ("zb", 0, 128), 0.0)
+    for k in range(2):
+        act(("jv", 128 * k, 128 * k + 128), ("ji", 0, 128), pg[14 + k])
+    act(pg[12], pd4, 0.0, 32.0)
+    act(pg[13], pd4, 16.0, 32.0)
+    for k in range(2):
+        act(("l4", 6 + 2 * k, 8 + 2 * k), ("zb", 0, 2), pg[12 + k])
+    act(pg[10], p16, 0.0, 4.0)
+    act(("kn", 0, 1), p4, float(N - s))
+    act(pg[11], pd8, pg[10], -32.0)
+    act(pg[0], pd16, 1.0, -1.0)
     quarter(2)
     score(2)
+    half0[0]()
     quarter(3)
-    if s < N - 1:
-        border(T.cores[s + 1], X1 - 2, X1 - 8, "bq", 14, "bz", 8, "lrecv")
+    if 0 < s < N - 1:
+        border(T.cores[s + 1], "xq", X1 - 2, "xz", X1 - 8, "bq", 14, "bz", 8, "lrecv")
     if s:
         arrives("lrecv", len(shared(T.cores[s - 1], [core])), [("bq", 14, 16), ("bz", 8, 16)])
     score(3)
     if s < N - 1:
         mm("pwx", "pq", "pz", 16, "xq", "xz", X1 + 2 - 128, 128)
-    half0[2]()
-    ts(("l4", 0, 2), ("zb", 0, 2), pg[6], pg[8], ALU.add, ALU.add)
-    half0[3]()
+    half0[1]()
     half1[0]()
-    ts(("mb", 0, 32), ("tq", 0, 32), pg[1], -BIG, ALU.is_equal, ALU.mult)
+    half0[2]()
     half1[1]()
-    cp(("lg16", 0, 4), ("l4", 0, 4))
+    half0[3]()
     half1[2]()
+    cp(("lg16", 0, 6), ("l4", 0, 6))
+    right[0]()
     half1[3]()
+    right[1]()
 
     pick("v", ("la", 0, 64), ("cc", 0, CC), "lg16", 0, 4)
-    right[0]()
-    tr(("lr", 0, 64), ("la", 0, 64))
-    right[1]()
-    tt(("eq", 0, 32), ("lr", 32, 64), ("lr", 31, 63), ALU.is_equal)
     right[2]()
-    scan(("cn", 0, 64), ("eq", 0, 64), ("one", 0, 64), 0.0, ALU.add, ALU.subtract)
+    tr(("lr", 0, 64), ("la", 0, 64))
     right[3]()
+    tt(("eq", 0, 32), ("lr", 32, 64), ("lr", 31, 63), ALU.is_equal)
+    n = 64
+    if s < N - 1:
+        n = 96
+        ts(("eq", 64, 65), ("lr", 63, 64), ("bc", 15, 16), ("sl", 0, 1), ALU.is_equal, ALU.max)
+    scan(("cn", 0, n), ("eq", 0, n), ("one", 0, n), 0.0, ALU.add, ALU.subtract)
     tt(("nk", 0, 32), ("eq", 0, 32), ("kd", 0, 32), ALU.mult)
-    tr(("rw", 0, 32), ("cn", 32, 64))
-    if s < N - 1:
-        ts(("cf", 0, 32), ("zb", 0, 32), ("bc", 15, 16), ("lr", 63, 64), ALU.add, ALU.is_equal)
-    tt(("xa", 0, 32), ("nk", 0, 32), ("cn", 0, 32), ALU.add)
-    scan(("sf", 0, 16), ("sm", 0, 16), ("rw", 0, 16), 0.0, ALU.mult, ALU.add)
-    if s < N - 1:
-        tr(("ct", 0, 32), ("cf", 0, 32))
+    tr(("rw", 0, n - 32), ("cn", 32, n))
+    tt(("xa", 0, 32), ("nk", 0, 32), ("cn", 0, 32), ALU.subtract)
     own = ("sf", 15, 16)
     nn = ("col", 2, 3)
-    total(nn, ("rw", 0, 16), 16)
-    ts(("of16", 0, 32), ("xa", 0, 32), own, None, ALU.subtract)
-    later = [T.cores[d] for d in range(s + 1, N)]
+    later = sorted((T.cores[d] for d in range(s + 1, N)), key=lambda d: topo.same_plane(topo.chip(core), topo.chip(d)))
     if later:
-        scan(("msg", 0, 16), ("rw", 0, 16), ("zb", 0, 16), ("ct", 31, 32), ALU.add, ALU.add)
+        scan(("msg", 0, 16), ("rw", 48, 64), ("zb", 0, 16), 1.0, ALU.add, ALU.add)
+    scan(("sf", 0, 16), ("sm", 0, 16), ("rw", 0, 16), 0.0, ALU.mult, ALU.add)
+    if later:
         eng = shared(core, later)
         remote(lambda: g.remote_dma_fused([RemoteDMATransfer(dst_ids=[where(d) for d in later], dma_engine_mask=mask(eng), remote_sem=T.sem.mrecv,
                                                              srcs=[A("msg", 15, 16)], dsts=[A("msgin", s, s + 1) for _ in later])],
                                           local_sem=T.sem.mloc), [("msg", 15, 16)], "mloc", len(eng))
+    total(nn, ("rw", 0, 16), 16)
+    cp(("lg16", 6, 10), ("l4", 6, 10))
+    pick("v", ("of16", 0, 16), ("xa", 0, 32), "lg16", 4, 5, own, float(W0 + 127))
     if s:
         arrives("mrecv", sum(len(shared(T.cores[r], [T.cores[d] for d in range(r + 1, N)])) for r in range(s)), [("msgin", 0, s)])
-    dma("s", "dw", A("wb", 0, 512), T.w[:, 0:512], [("msg", 15, 16), ("of16", 0, 32)], [("wb", 0, 512)])
+    dma("s", "dw", A("wb", 0, 512), T.w[:, 0:512], [("msg", 15, 16), ("of16", 0, 16)], [("wb", 0, 512)])
     dma("s", "dv", A("vb", 0, 512), T.v[:, 0:512], [], [("vb", 0, 512)])
-    act(("kn2", 0, 2), ("kn", 0, 2), nn)
-    emit("v", lambda: g.vector.tensor_copy(T.fw[:, 0:FW].indirect(T.of16[:, 0:32]), A("jv", 0, 512)),
-         [("jv", 0, 512), ("of16", 0, 32)], [("fw", 0, FW)])
+    act(("kn2", 0, 1), nn, ("kn", 0, 1), -1.0)
+    emit("v", lambda: g.vector.tensor_copy(T.fw[:, 0:FW].indirect(T.of16[:, 0:16]), A("jv", 0, 256)),
+         [("jv", 0, 256), ("of16", 0, 16)], [("fw", 0, FW)])
+    tr(("ft", 0, 128), ("fw", W0, W0 + 128))
+    pick("v", ("fa", 0, 64), ("ft", 0, 128), "lg16", 6, 10)
+    m = [("msgin", r, r + 1) for r in range(s)]
+    z = ("kn2", 0, 1)
+    if s == 3:
+        ts(("kn2", 1, 2), z, m.pop(), None, ALU.subtract)
+        z = ("kn2", 1, 2)
+    tt(("fb", 0, 32), ("fa", 0, 32), ("fa", 32, 64), ALU.max)
+    if len(m) == 2:
+        ts(("zi16", 0, 1), z, m[0], m[1], ALU.subtract, ALU.subtract)
+    elif m:
+        ts(("zi16", 0, 1), z, m[0], None, ALU.subtract)
+    else:
+        cp(("zi16", 0, 1), z)
+    tr(("fm", 0, 32), ("fb", 0, 32))
+    pick("v", ("off16", 0, 16), ("tab", 0, TAB), "zi16", 0, 1, pg[11])
+    pick("v", ("ls16", 0, 64), ("fm", 0, 32), "off16", 0, 4, p4)
+
+    def gather(q, a, b):
+        c = 8 + a // 4 + 16 * (a >= 2 * G)
+        pick(q, ("xb", SX + 4 * a, SX + 4 * b), ("xb", XB, SX), "ls16", c, c + (b - a) // 4)
+
+    def send(ks, sign, cq, cz, width, src, land, rsem, lsem):
+        peers = [T.cores[(s + sign * k) % N] for k in ks]
+        eng = shared(core, peers)
+        q = len(eng) // 4
+        cuts = {1: [(0, 4)], 2: [(0, 2), (2, 4)], 3: [(0, 2), (2, 3), (3, 4)]}[len(ks)]
+        for codes in (True, False):
+            moves = []
+            for k, d, (e0, e1) in zip(ks, peers, cuts if codes else [(4 - b, 4 - a) for a, b in cuts[::-1]] if len(ks) == 3 else cuts):
+                a, b = src(k), land(k)
+                if codes:
+                    x, y = A(cq, a, a + width).bitcast(dt.uint8), A(cq, b, b + width).bitcast(dt.uint8)
+                else:
+                    x, y = A(cz, a, a + width), A(cz, b, b + width)
+                moves.append(RemoteDMATransfer(dst_ids=[where(d)], dma_engine_mask=mask(eng[q * e0:q * e1]), remote_sem=T.sem[rsem], srcs=[x], dsts=[y]))
+            lo, hi = src(ks[0]), src(ks[-1]) + width
+            remote(lambda: g.remote_dma_fused(moves, local_sem=T.sem[lsem]), [(cq, lo, hi), (cz, lo, hi)], lsem, 4 * q)
+        return 8 * q
+
+    n1 = G * len(STAGES[0])
+    if len(STAGES) == 1:
+        gather("a", 2 * G, GT)
+        gather("v", 0, 2 * G)
+    else:
+        gather("a", n1 // 2, n1)
+        gather("v", 0, n1 // 2)
+        quant("cq", "cz", 0, "xb", SX // 4 + n1 - GT, GT)
+        n = send(STAGES[0], -1, "cq", "cz", G, lambda k: GT - n1 + G * (k - 1), lambda k: CL + G * (k - 1), "crecv0", "cloc")
+        arrives("crecv0", n, [(b, CL, CL + n1) for b in ("cq", "cz")])
+        if n1 < 2 * G:
+            gather("a", G, 2 * G)
+            gather("v", 2 * G, GT)
+        else:
+            gather("a", 2 * G, 3 * G)
+            gather("v", 3 * G, GT)
+    quant("cq", "cz", GT, "xb", SX // 4, GT)
+    for j, ks in enumerate(STAGES):
+        if j or len(STAGES) == 1:
+            n = send(ks, -1, "cq", "cz", G, lambda k: GT + G * (k - 1), lambda k: CL + G * (k - 1), "crecv%d" % j, "cloc")
+            arrives("crecv%d" % j, n, [(b, CL + G * (ks[0] - 1), CL + G * ks[-1]) for b in ("cq", "cz")])
+
+    def states(j):
+        if j >= len(STAGES):
+            return
+        ks = STAGES[j]
+        n = G * (len(ks) + (j == 0))
+        e = 4 * (GT - n1 + G * ks[-1])
+        for i in range(4):
+            mm("pa%d" % i, "aq", "az", 128 * i, "cq", "cz", CL + G * ks[-1] - GT, GT)
+        for i in range(4):
+            o = ("hb", e - 4 * n + i, e, 4)
+            r, w = [("pa%d" % i, 0, 512)], [("hb", 4 * j + i + 1, 4 * j + i + 2)]
+            if i % 2 == 0:
+                emit("a", lambda: g.scalar.activation(ap(o), A("pa%d" % i, GT - n, GT), ACT.Relu, scale=0.05), r, w)
+            else:
+                emit("v", lambda: g.vector.tensor_scalar(ap(o), A("pa%d" % i, GT - n, GT), 0.0, 0.05, ALU.max, ALU.mult), r, w)
+        a = GT * (j + 3 - len(STAGES))
+        emit("v", lambda: g.vector.quantize_mx(A("hq", a, a + GT), A("hz", a, a + GT), A("hb", e - 4 * GT, e)),
+             [("hb", 0, 4 * j + 5)], [("hq", a, a + GT), ("hz", a, a + GT)])
+        n = send(ks, 1, "hq", "hz", GB, lambda k: a + GT - GB - G * (ks[-1] - k), lambda k: HL + GB * (k - 1), "hrecv%d" % j, "hloc")
+        arrives("hrecv%d" % j, n, [(b, HL + GB * (ks[0] - 1), HL + GB * ks[-1]) for b in ("hq", "hz")])
 
     Y = ("msgin", 0, 1)
     if s > 1:
         Y = ("col", 0, 1)
         total(Y, ("msgin", 0, s), s)
-
-    def wrap(k):
-        scan(("fm", 32 * k, 32 * k + 32), ("mb", 0, 32), ("fw", k, 128, 4), 0.0, ALU.add, ALU.max)
-
-    if s:
-        ts(("vi", 0, 2), ("kn2", 0, 2), Y, -1.0, ALU.add, ALU.mult)
-    else:
-        ts(("vi", 0, 2), ("kn2", 0, 2), -1.0, None, ALU.mult)
-    wrap(0)
-    wrap(1)
-    ts(("ci", 0, 2), ("vi", 0, 2), 3, None, ALU.bitwise_and)
-    wrap(2)
-    wrap(3)
-    ts(("off16", 0, 2), ("ci", 0, 2), 32.0, pg[11], ALU.mult, ALU.add)
-    pick("v", ("ls16", 0, 32), ("fm", 0, 128), "off16", 0, 2)
-    pick("a", ("sx", 288, 4 * GT), ("xb", XB, XB + 2048), "ls16", 18, 32)
-    pick("v", ("sx", 0, 288), ("xb", XB, XB + 2048), "ls16", 0, 18)
-    quant("cq", "cz", 0, "sx", 0, GT)
-
-    peers = [T.cores[(s + i) % N] for i in (1, 2, 3)]
-    eng = shared(core, peers)
-    q = len(eng) // 4
-    code_eng = [eng[0:2 * q], eng[2 * q:3 * q], eng[3 * q:4 * q]]
-    scale_eng = [eng[0:q], eng[q:2 * q], eng[2 * q:4 * q]]
-
-    def hop(cq, cz, width, src, land, rsem, lsem):
-        for codes in (True, False):
-            moves = []
-            for i in (1, 2, 3):
-                a, b = src(i), land(i)
-                if codes:
-                    x, y = A(cq, a, a + width).bitcast(dt.uint8), A(cq, b, b + width).bitcast(dt.uint8)
-                else:
-                    x, y = A(cz, a, a + width), A(cz, b, b + width)
-                moves.append(RemoteDMATransfer(dst_ids=[where(peers[i - 1])], dma_engine_mask=mask((code_eng if codes else scale_eng)[i - 1]),
-                                               remote_sem=T.sem[rsem], srcs=[x], dsts=[y]))
-            lo, hi = src(1), src(3) + width
-            remote(lambda: g.remote_dma_fused(moves, local_sem=T.sem[lsem]), [(cq, lo, hi), (cz, lo, hi)], lsem, 4 * q)
-
-    hop("cq", "cz", G, lambda i: G * (i - 1), lambda i: LAND + G * (3 - i), "crecv", "cloc")
-    arrives("crecv", 8 * q, [("cq", LAND, LAND + 3 * G), ("cz", LAND, LAND + 3 * G)])
-
     left = [lambda: None] * 4
     if s:
         quant("bq", "bz", 16, "xb", XB // 4, 128)
@@ -379,23 +441,25 @@ def rank_program(g, core, T, topo):
         left = argmax("pl1", 0, 32, edge)
         act(("be", 32, 64), ("zb", 0, 32), ("lr", 32, 33))
     act(("lb0", 0, 32), ("lr", 32, 64), 15.0, -1.0)
-    quant("aq", "az", 0, "ab", 0, 512)
-    left[0]()
     quant("wq", "wz", 0, "wb", 0, 128)
     mm("pwx", "wq", "wz", 0, "xq", "xz", X0, 512)
-    left[1]()
-    quant("vq", "vz", 0, "vb", 0, 128)
-    left[2]()
+    quant("aq", "az", 0, "ab", 0, 512)
+    left[0]()
     nE = ("col", 1, 2)
     ts(("u", 0, 32), ("cn", 0, 32), own, None, ALU.subtract)
+    left[1]()
     if s:
         ts(nE, nn, Y, 1.0, ALU.add, ALU.add)
     else:
         ts(nE, nn, 1.0, None, ALU.add)
+    left[2]()
+    quant("vq", "vz", 0, "vb", 0, 128)
     left[3]()
     if s:
         act(("be", 0, 32), ("zb", 0, 32), ("bc", 15, 16))
     cp(("wx", 0, 512), ("pwx", 0, 512), "a")
+    if len(STAGES) > 1:
+        states(0)
     ts(("t1", 0, 16), ("u", 0, 16), pg[0], None, ALU.mult)
     ts(("t2", 0, 16), ("u", 16, 32), pd16, None, ALU.mult)
     ts(("lb1", 0, 32), ("u", 0, 32), nE, -1.0, ALU.add, ALU.mult)
@@ -406,31 +470,24 @@ def rank_program(g, core, T, topo):
     tr(("ut", 0, 32), ("in2", 0, 32))
     dma("s", "dl0", T.lb[0:1, :], T.lb0[0:16, :], [("lb0", 0, 32)], [])
     dma("s", "dl1", T.lb[1:2, :], T.lb1[0:16, :], [("lb1", 0, 32)], [])
+    if len(STAGES) == 1:
+        states(0)
+    states(1)
+    states(2)
 
-    for i in range(4):
-        mm("pa%d" % i, "aq", "az", 128 * i, "cq", "cz", 3 * G, GT)
-    for i in range(4):
-        o = ("hb", i, 4 * GT, 4)
-        r, w = [("pa%d" % i, 0, 512)], [("hb", i * 4 * GT, i * 4 * GT + 1)]
-        if i % 2 == 0:
-            emit("a", lambda: g.scalar.activation(ap(o), A("pa%d" % i, 0, GT), ACT.Relu, scale=0.05), r, w)
-        else:
-            emit("v", lambda: g.vector.tensor_scalar(ap(o), A("pa%d" % i, 0, GT), 0.0, 0.05, ALU.max, ALU.mult), r, w)
-    emit("v", lambda: g.vector.quantize_mx(A("hq", 0, GT), A("hz", 0, GT), A("hb", 0, 4 * GT)), [("hb", 0, 16 * GT)], [("hq", 0, GT), ("hz", 0, GT)])
-    hop("hq", "hz", GB, lambda i: G * i - 2, lambda i: LAND + GB * (i - 1), "hrecv", "hloc")
-    arrives("hrecv", 8 * q, [("hq", LAND, LAND + 3 * GB), ("hz", LAND, LAND + 3 * GB)])
-
-    mm("pv", "vq", "vz", 0, "hq", "hz", 0, GT)
+    mm("pv", "vq", "vz", 0, "hq", "hz", 2 * GT, GT)
     cp(("hv", 2, GB), ("pv", 0, G), "a")
     cp(("hv", 0, 2), ("pv", GT - 2, GT), "a")
     for d in range(2):
         emit("v", lambda: g.vector.tensor_copy(T.wi[:, d:32:2], A("ut", 16 * d, 16 * d + 16)), [("ut", 0, 32)], [("wi", 16 * d, 16 * d + 16)])
-    ts(("ki", 0, 32), ("wi", 0, 32), 2, None, ALU.logical_shift_right)
+    ts(("wv", 0, 32), ("wi", 0, 32), -1.0, 159.0, ALU.mult, ALU.add)
     ts(("zi", 0, 32), ("wi", 0, 32), nE, float(s + 1024), ALU.add, ALU.add)
+    ts(("ki", 0, 32), ("wv", 0, 32), 28, None, ALU.bitwise_and)
+    ts(("kj", 0, 32), ("wv", 0, 32), 5, None, ALU.logical_shift_right)
     if s:
         ts(("cm", 0, 32), ("wi", 0, 32), nn, -1.0, ALU.add, ALU.is_equal)
         ts(("col", 3, 4), ("br", 1, 2), ("br", 32, 33), -1.0, ALU.is_equal, ALU.mult)
-    ts(("gf", 0, 32), ("ki", 0, 32), -1.0, float(G), ALU.mult, ALU.add)
+    tt(("gf", 0, 32), ("ki", 0, 32), ("kj", 0, 32), ALU.add)
     ts(("bi", 0, 32), ("zi", 0, 32), 3, None, ALU.bitwise_and)
     if s:
         ts(("cm", 0, 32), ("cm", 0, 32), ("col", 3, 4), 1.0, ALU.mult, ALU.add)
@@ -440,7 +497,7 @@ def rank_program(g, core, T, topo):
     tt(("ix", 0, 32), ("gx" if s else "gf", 0, 32), ("bf", 0, 32), ALU.add)
     cp(("ix16", 0, 32), ("ix", 0, 32))
 
-    mm("pl0", "vq", "vz", 0, "hq", "hz", LAND + 3 * GB - 128, 128)
+    mm("pl0", "vq", "vz", 0, "hq", "hz", HL + 3 * GB - 128, 128)
     cp(("hv", GB, 4 * GB), ("pl0", 128 - 3 * GB, 128))
     for k, (c, d) in enumerate(((0, 160), (160, 352), (352, 512))):
         emit("v", lambda: g.vector.tensor_tensor(A("yb", c, d), T.hv[:, 0:4 * GB].indirect(T.ix16[:, c // 16:d // 16]), A("wx", c, d), ALU.add),

@@ -7,8 +7,8 @@ N = 4
 G = 32
 GT = 4 * G
 GB = G + 2
-CL = 2 * GT
-HL = 3 * GT
+CL = 3 * GT
+HL = 2 * GT
 SX = 16 + 2048
 X0 = 16
 X1 = X0 + 512
@@ -17,26 +17,28 @@ BIG = 1e25
 W0 = 32
 FW = 800
 TAB = 528
+YS = 256
 CC = 272
-STAGES = ((1, 2, 3),)
 
 SCRATCH = {}
 for _dtype, _names in {
-    "bfloat16": "pb 64 pt 576 xb 2576 ab 2048 wb 512 vb 512 nn 256 cc 272 la 64 lr 64 msg 16 msgin 8 bn 16 bc 16 hb 768 tab 528 sl 8 eb 512",
-    "float32": "zb 136 sc 256 rs 136 xm 264 eq 96 one 96 cn 96 nk 32 xa 32 rw 64 sf 16 sm 16 bs 32 bx 24 be 64 br 64 pf 16 pg 16 l4 16 "
-               "row 32 kn 8 kn2 8 kd 32 ji 128 jv 256 fw 800 ft 128 fa 64 fb 32 fm 32 yj 16 col 8 u 32 t1 16 t2 16 in2 32 ut 32 gf 32 cm 32 gx 32 "
+    "bfloat16": "pb 64 pt 576 xb 2576 ab 2048 wb 512 vb 512 nn 256 cc 272 la 64 lr 64 msg 16 msgin 8 bn 48 bc 48 hb 640 tab 528 eb 512",
+    "float32": "sc 256 rs 136 xm 264 eq 64 one 64 cn 128 nk 32 xa 32 rw 96 mt 16 sf 16 sm 16 bs 64 bx 64 be 64 pf 16 pg 16 l4 16 "
+               "row 32 kn 8 kn2 8 kd 32 ji 128 jv 256 fw 800 fm 32 yj 64 col 16 in2 32 ut 32 gf 32 cm 32 gx 32 "
                "bf 32 ix 32 hv 136 wx 512 yb 512 lb0 32 lb1 32",
     "int32": "pi 12 wi 32 wv 32 zi 32 bi 32 ki 32 kj 32",
     "uint16": "lg16 16 of16 16 zi16 2 off16 16 ls16 64 ix16 32",
-    "float8_e4m3fn_x4": "pq 144 xq 544 bq 144 aq 512 wq 128 vq 128 cq 352 hq 488 nq 128",
-    "uint8": "pz 144 xz 544 bz 144 az 512 wz 128 vz 128 cz 352 hz 488 nz 128",
+    "float8_e4m3fn_x4": "pq 144 xq 544 aq 512 wq 128 vq 128 cq 480 hq 360 nq 128",
+    "uint8": "pz 144 xz 544 az 512 wz 128 vz 128 cz 576 hz 464 nz 128",
 }.items():
     _l = _names.split()
     for _n, _w in zip(_l[::2], _l[1::2]):
         SCRATCH[_n] = ("sbuf", [128, int(_w)], _dtype)
+SCRATCH["ft"] = ("sbuf", [128, 4, 32], "float32")
+SCRATCH["fb"] = ("sbuf", [128, 8, 4], "float32")
 for _n in ("pl0", "pl1", "pwx", "pa0", "pa1", "pa2", "pa3", "pv"):
     SCRATCH[_n] = ("psum", [128, 512], "float32")
-SEMAPHORES = ["sv", "sa", "st", "sg", "lrecv", "rrecv", "bnq", "bxq", "mrecv", "mloc", "crecv0", "crecv1", "crecv2", "cloc", "hrecv0", "hrecv1", "hrecv2", "hloc",
+SEMAPHORES = ["sv", "sa", "st", "sg", "lrecv", "rrecv", "bnq", "mrecv0", "mrecv1", "mrecv2", "mloc", "crecv0", "crecv1", "cloc", "hrecv0", "hrecv1", "hloc",
               "dp", "de", "dx0", "dx1", "dx2", "dx3", "da", "dw", "dv", "dl0", "dl1", "dy0", "dy1", "dy2"]
 
 
@@ -104,11 +106,11 @@ def rank_program(g, core, T, topo):
     def A(name, a, b):
         return T[name][:, a:b]
 
-    def ap(t):
-        return T[t[0]][:, t[1]:t[2]:t[3]] if len(t) > 3 else T[t[0]][:, t[1]:t[2]]
-
     def span(t):
-        return (t[0], t[1], t[2])
+        return ("eb", t[1] + 32, t[2] + 32) if t[0] == "zb" else (t[0], t[1], t[2])
+
+    def ap(t):
+        return T[t[0]][:, t[1]:t[2]:t[3]] if len(t) > 3 else A(*span(t))
 
     def dma(q, sem, out, in_, reads, writes):
         eng = g.sync if q == "s" else g.scalar
@@ -186,27 +188,26 @@ def rank_program(g, core, T, topo):
         return DstId(rid=rid, pnc=pid)
 
     dma("a", "dp", A("pb", 0, 64), T.p[:, 0:64], [], [("pb", 0, 64)])
-    dma("s", "de", A("eb", 24, 32), T.x[:, 0:8] if s else T.x[:, 2040:2048], [], [("eb", 24, 32)])
+    dma("s", "de", A("eb", 24, 32), T.x[:, 0:8] if s == N - 1 else T.x[:, 2040:2048], [], [("eb", 24, 32)])
     for k, que in enumerate("sasa"):
         c = XB + 512 * k
         dma(que, "dx%d" % k, A("xb", c, c + 512), T.x[:, 512 * k:512 * k + 512], [], [("xb", c, c + 512)])
-    dma("s", "da", A("ab", 0, 2048), T.a[:, 0:2048], [], [("ab", 0, 2048)])
+    for n, w in (("a", 2048), ("w", 512), ("v", 512)):
+        dma("s", "d" + n, A(n + "b", 0, w), T[n][:, 0:w], [], [(n + "b", 0, w)])
 
     iota(("pi", 0, 2), [[-15, 2]], 15, 1)
     iota(("row", 0, 16), [[1, 16]], 0)
     iota(("ji", 0, 128), [[4, 8], [128, 16]], 0)
     iota(("kd", 0, 32), [[1, 32]], 129)
-    fill(("zb", 0, 136), 0.0)
-    fill(("eb", 0, 24), 0.0)
     fill(("eb", 32, 512), 0.0)
+    fill(("eb", 0, 24), 0.0)
     fill(("pt", 0, 576), 0.0)
-    if len(STAGES) > 1:
-        emit("v", lambda: g.vector.memset(A("hb", 0, 8 * G), 0.0), [], [("hb", 0, 1)])
     act(("rs", 0, 136), ("zb", 0, 136), BIG)
     for o, c in ((2, 15), (4, 3)):
         ts(("pi", o, o + 2), ("pi", 0, 2), c, None, ALU.bitwise_and)
     for o, c, d in ((6, 2, 3), (8, 3, 1), (10, 4, 1)):
         ts(("pi", o, o + 2), ("pi", 0, 2), c, d, ALU.logical_shift_right, ALU.bitwise_and)
+    cp(("pf", 0, 10), ("pi", 2, 12))
 
     def border(d, xq, a, xz, za, bq, b, bz, zb, rsem):
         e = shared(core, [d])
@@ -219,17 +220,16 @@ def rank_program(g, core, T, topo):
         return len(e)
 
     quant("nq", "nz", 0, "eb", 0, 128)
-    if s:
-        n = border(T.cores[s - 1], "nq", 5, "nz", 5, "xq", X1, "xz", X1, "rrecv")
+    if s == N - 1:
+        border(T.cores[s - 1], "nq", 5, "nz", 5, "xq", X1, "xz", X1, "rrecv")
     else:
-        n = border(T.cores[1], "nq", 6, "nz", 0, "bq", 14, "bz", 8, "lrecv")
+        border(T.cores[s + 1], "nq", 6, "nz", 0, "xq", X0 - 2, "xz", X0 - 8, "lrecv")
     iota(("tab", 0, TAB), [[0, TAB // 4], [-1, 4]], 3)
     for k in range(4):
         cp(("pt", 64 + 128 * k, 128 + 128 * k), ("pb", 0, 64), "va"[k // 2])
     act(("rs", 0, 136, 16), ("zb", 0, 9), -BIG)
     act(("xm", 0, 1), ("zb", 0, 1), -BIG)
-    act(("bx", 0, 1), ("zb", 0, 1), -BIG)
-    quant("pq", "pz", 0, "pt", 0, 144)
+    act(("bx", 0, 64), ("zb", 0, 64), -BIG)
 
     def argmax(pl, c, n, bufs):
         sc, xm, nn_, cc, o, w = bufs
@@ -244,23 +244,20 @@ def rank_program(g, core, T, topo):
     def score(c):
         mm("pl%d" % (c // 2), "pq", "pz", 16 - 16 * (c % 2), "xq", "xz", X0 + 128 * c, 128, c % 2 == 0, c % 2 == 1)
 
-    edge = ("bs", "bx", "bn", "bc", 0, 16)
     half0 = argmax("pl0", 0, 128, ("sc", "xm", "nn", "cc", 0, 128))
     half1 = argmax("pl1", 0, 128, ("sc", "xm", "nn", "cc", 128, 128))
-    right = argmax("pwx", 96, 32, edge) if s < N - 1 else [lambda: None] * 4
+    guests = [("pv", 1, 2)] * (s > 0) + [("pwx", 127, 128)] * (s == N - 2)
 
     quarter(0)
-    if s < N - 1:
-        arrives("rrecv", len(shared(T.cores[s + 1], [core])), [("xq", X1, X1 + 2), ("xz", X1, X1 + 8)])
+    quant("pq", "pz", 0, "pt", 0, 144)
     score(0)
     quarter(1)
     score(1)
-    cp(("pf", 0, 10), ("pi", 2, 12))
     p16, p4, pd4, pd8, pd16 = [("pf", k, k + 1) for k in (1, 3, 5, 7, 9)]
     pg = [("pg", k, k + 1) for k in range(16)]
     act(("cc", 256, CC), ("zb", 0, CC - 256), -1.0)
-    act(("one", 0, 96), ("zb", 0, 96), 1.0)
-    act(("eq", 32, 96), ("zb", 0, 64), 1.0)
+    act(("one", 0, 64), ("zb", 0, 64), 1.0)
+    act(("eq", 32, 64), ("zb", 0, 32), 1.0)
     act(pg[8], p16, 1.0, -1.0, ACT.Relu)
     act(pg[3], ("pf", 3, 4), 15.0, 32.0)
     act(pg[8], pg[8], 15.0)
@@ -274,7 +271,6 @@ def rank_program(g, core, T, topo):
     act(("l4", 0, 2), ("zb", 0, 2), pg[6])
     act(pg[9], p16, 0.0, 32.0)
     act(("l4", 4, 6), ("zb", 0, 2), pg[1])
-    act(("sl", 0, 1), p16, 15.0, -1.0, ACT.Sign)
     act(("kd", 0, 32), ("kd", 0, 32), pg[9])
     act(("sm", 0, 16), ("row", 0, 16), p16, -1.0, ACT.Sign)
     act(pg[14], pd16, 0.0, 64.0)
@@ -283,24 +279,16 @@ def rank_program(g, core, T, topo):
     act(("fw", W0, W0 + 128), ("zb", 0, 128), 0.0)
     for k in range(2):
         act(("jv", 128 * k, 128 * k + 128), ("ji", 0, 128), pg[14 + k])
-    act(pg[12], pd4, 0.0, 32.0)
-    act(pg[13], pd4, 16.0, 32.0)
-    for k in range(2):
-        act(("l4", 6 + 2 * k, 8 + 2 * k), ("zb", 0, 2), pg[12 + k])
-    act(pg[10], p16, 0.0, 4.0)
-    act(("kn", 0, 1), p4, float(N - s))
-    act(pg[11], pd8, pg[10], -32.0)
-    act(pg[0], pd16, 1.0, -1.0)
     quarter(2)
     score(2)
-    half0[0]()
     quarter(3)
-    if 0 < s < N - 1:
-        border(T.cores[s + 1], "xq", X1 - 2, "xz", X1 - 8, "bq", 14, "bz", 8, "lrecv")
-    if s:
-        arrives("lrecv", len(shared(T.cores[s - 1], [core])), [("bq", 14, 16), ("bz", 8, 16)])
     score(3)
-    if s < N - 1:
+    half0[0]()
+    if s:
+        arrives("lrecv", len(shared(T.cores[s - 1], [core])), [("xq", X0 - 2, X0), ("xz", X0 - 8, X0)])
+        mm("pv", "pq", "pz", 16, "xq", "xz", X0 - 2, 128)
+    if s == N - 2:
+        arrives("rrecv", len(shared(T.cores[s + 1], [core])), [("xq", X1, X1 + 2), ("xz", X1, X1 + 8)])
         mm("pwx", "pq", "pz", 16, "xq", "xz", X1 + 2 - 128, 128)
     half0[1]()
     half1[0]()
@@ -309,114 +297,108 @@ def rank_program(g, core, T, topo):
     half0[3]()
     half1[2]()
     cp(("lg16", 0, 6), ("l4", 0, 6))
-    right[0]()
     half1[3]()
-    right[1]()
 
+    later = sorted((T.cores[d] for d in range(N - 1, s, -1)), key=lambda d: topo.same_plane(topo.chip(core), topo.chip(d)))
     pick("v", ("la", 0, 64), ("cc", 0, CC), "lg16", 0, 4)
-    right[2]()
     tr(("lr", 0, 64), ("la", 0, 64))
-    right[3]()
+    ng = len(guests)
+    for k, c in enumerate(guests):
+        ts(("be", 32 * k, 32 * k + 32), ("zb", 0, 32), c, None, ALU.subtract)
+        act(("cn", 64 + 32 * k, 96 + 32 * k), ("zb", 0, 32), ("lr", 32 + 31 * k, 33 + 31 * k))
     tt(("eq", 0, 32), ("lr", 32, 64), ("lr", 31, 63), ALU.is_equal)
-    n = 64
-    if s < N - 1:
-        n = 96
-        ts(("eq", 64, 65), ("lr", 63, 64), ("bc", 15, 16), ("sl", 0, 1), ALU.is_equal, ALU.max)
-    scan(("cn", 0, n), ("eq", 0, n), ("one", 0, n), 0.0, ALU.add, ALU.subtract)
+    if ng:
+        tr(("bs", 0, 32 * ng), ("be", 0, 32 * ng))
+    scan(("cn", 0, 64), ("eq", 0, 64), ("one", 0, 64), 0.0, ALU.add, ALU.subtract)
+    for k in range(ng):
+        c = 32 * k
+        scan(("bx", c, c + 16), ("bs", c, c + 16), ("bs", c, c + 16), BIG, ALU.min, ALU.min)
+        emit("a", lambda: g.scalar.activation(A("yj", c, c + 31), A("bx", c, c + 31), ACT.Sign, bias=A("bx", c + 15, c + 16), scale=-1.0,
+                                              accum_out=A("col", 9 + k, 10 + k)), [("bx", c, c + 31)], [("yj", c, c + 31), ("col", 9 + k, 10 + k)])
+    tr(("rw", 0, 32 + 32 * ng), ("cn", 32, 64 + 32 * ng))
     tt(("nk", 0, 32), ("eq", 0, 32), ("kd", 0, 32), ALU.mult)
-    tr(("rw", 0, n - 32), ("cn", 32, n))
-    tt(("xa", 0, 32), ("nk", 0, 32), ("cn", 0, 32), ALU.subtract)
+    nn = ("mt", 15, 16)
     own = ("sf", 15, 16)
-    nn = ("col", 2, 3)
-    later = sorted((T.cores[d] for d in range(s + 1, N)), key=lambda d: topo.same_plane(topo.chip(core), topo.chip(d)))
-    if later:
-        scan(("msg", 0, 16), ("rw", 48, 64), ("zb", 0, 16), 1.0, ALU.add, ALU.add)
+    msg = ("msg", 15, 16)
+    true = msg if s < 2 else ("col", 8, 9)
+    scan(("mt" if s else "msg", 0, 16), ("rw", 0, 16), ("zb", 0, 16), 0.0, ALU.add, ALU.add)
+    if s == 0:
+        nn = msg
     scan(("sf", 0, 16), ("sm", 0, 16), ("rw", 0, 16), 0.0, ALU.mult, ALU.add)
+    if s:
+        ts(true, ("col", 9, 10), ("rw", 32, 33), nn, ALU.is_equal, ALU.add)
+    tt(("xa", 0, 32), ("nk", 0, 32), ("cn", 0, 32), ALU.subtract)
+    if s == N - 2:
+        ts(msg, ("col", 10, 11), ("rw", 79, 80), true, ALU.is_equal, ALU.add)
+    pick("v", ("of16", 0, 16), ("xa", 0, 32), "lg16", 4, 5, own, float(W0 + 127))
+    mine = nn if s == N - 1 else true
     if later:
         eng = shared(core, later)
-        remote(lambda: g.remote_dma_fused([RemoteDMATransfer(dst_ids=[where(d) for d in later], dma_engine_mask=mask(eng), remote_sem=T.sem.mrecv,
+        remote(lambda: g.remote_dma_fused([RemoteDMATransfer(dst_ids=[where(d) for d in later], dma_engine_mask=mask(eng), remote_sem=T.sem["mrecv%d" % s],
                                                              srcs=[A("msg", 15, 16)], dsts=[A("msgin", s, s + 1) for _ in later])],
                                           local_sem=T.sem.mloc), [("msg", 15, 16)], "mloc", len(eng))
-    total(nn, ("rw", 0, 16), 16)
-    cp(("lg16", 6, 10), ("l4", 6, 10))
-    pick("v", ("of16", 0, 16), ("xa", 0, 32), "lg16", 4, 5, own, float(W0 + 127))
-    if s:
-        arrives("mrecv", sum(len(shared(T.cores[r], [T.cores[d] for d in range(r + 1, N)])) for r in range(s)), [("msgin", 0, s)])
-    dma("s", "dw", A("wb", 0, 512), T.w[:, 0:512], [("msg", 15, 16), ("of16", 0, 16)], [("wb", 0, 512)])
-    dma("s", "dv", A("vb", 0, 512), T.v[:, 0:512], [], [("vb", 0, 512)])
-    act(("kn2", 0, 1), nn, ("kn", 0, 1), -1.0)
+    for r in range(s):
+        arrives("mrecv%d" % r, len(shared(T.cores[r], T.cores[r + 1:])), [("msgin", r, r + 1)])
+    act(("kn", 0, 1), p4, float(N - s))
+    act(pg[10], p16, 0.0, 4.0)
+    act(("kn2", 0, 1), mine, ("kn", 0, 1), -1.0)
+    act(pg[11], pd8, pg[10], -32.0)
+    emit("a", lambda: g.scalar.activation(A("hb", 0, 4 * G), ap(("zb", 0, 4 * G)), ACT.Copy), [span(("zb", 0, 4 * G))], [("hb", 0, 1)])
     emit("v", lambda: g.vector.tensor_copy(T.fw[:, 0:FW].indirect(T.of16[:, 0:16]), A("jv", 0, 256)),
          [("jv", 0, 256), ("of16", 0, 16)], [("fw", 0, FW)])
-    tr(("ft", 0, 128), ("fw", W0, W0 + 128))
-    pick("v", ("fa", 0, 64), ("ft", 0, 128), "lg16", 6, 10)
+    emit("v", lambda: g.vector.transpose(T.ft[:, :, :], A("fw", W0, W0 + 128)), [("fw", W0, W0 + 128)], [("ft", 0, 128)])
     m = [("msgin", r, r + 1) for r in range(s)]
     z = ("kn2", 0, 1)
+    for h in range(2):
+        emit("v", lambda: g.vector.tensor_tensor(T.fb[:, 4 * h:4 * h + 4, :], T.ft[:, :, 0:4], T.ft[:, :, 16:20], ALU.max),
+             [("ft", 0, 128)], [("fb", 16 * h, 16 * h + 16)])
     if s == 3:
-        ts(("kn2", 1, 2), z, m.pop(), None, ALU.subtract)
-        z = ("kn2", 1, 2)
-    tt(("fb", 0, 32), ("fa", 0, 32), ("fa", 32, 64), ALU.max)
+        act(("kn2", 1, 2), m[0], z, -1.0)
+        z, m = ("kn2", 1, 2), m[1:]
     if len(m) == 2:
         ts(("zi16", 0, 1), z, m[0], m[1], ALU.subtract, ALU.subtract)
     elif m:
         ts(("zi16", 0, 1), z, m[0], None, ALU.subtract)
     else:
         cp(("zi16", 0, 1), z)
-    tr(("fm", 0, 32), ("fb", 0, 32))
+    emit("v", lambda: g.vector.transpose(A("fm", 0, 32), T.fb[:, :, :]), [("fb", 0, 32)], [("fm", 0, 32)])
     pick("v", ("off16", 0, 16), ("tab", 0, TAB), "zi16", 0, 1, pg[11])
-    pick("v", ("ls16", 0, 64), ("fm", 0, 32), "off16", 0, 4, p4)
+    pick("v", ("ls16", 0, 32), ("fm", 0, 32), "off16", 0, 2, p4)
 
     def gather(q, a, b):
         c = 8 + a // 4 + 16 * (a >= 2 * G)
         pick(q, ("xb", SX + 4 * a, SX + 4 * b), ("xb", XB, SX), "ls16", c, c + (b - a) // 4)
 
-    def send(ks, sign, cq, cz, width, src, land, rsem, lsem):
-        peers = [T.cores[(s + sign * k) % N] for k in ks]
-        eng = shared(core, peers)
-        q = len(eng) // 4
-        cuts = {1: [(0, 4)], 2: [(0, 2), (2, 4)], 3: [(0, 2), (2, 3), (3, 4)]}[len(ks)]
-        for codes in (True, False):
-            moves = []
-            for k, d, (e0, e1) in zip(ks, peers, cuts if codes else [(4 - b, 4 - a) for a, b in cuts[::-1]] if len(ks) == 3 else cuts):
-                a, b = src(k), land(k)
-                if codes:
-                    x, y = A(cq, a, a + width).bitcast(dt.uint8), A(cq, b, b + width).bitcast(dt.uint8)
-                else:
-                    x, y = A(cz, a, a + width), A(cz, b, b + width)
-                moves.append(RemoteDMATransfer(dst_ids=[where(d)], dma_engine_mask=mask(eng[q * e0:q * e1]), remote_sem=T.sem[rsem], srcs=[x], dsts=[y]))
-            lo, hi = src(ks[0]), src(ks[-1]) + width
-            remote(lambda: g.remote_dma_fused(moves, local_sem=T.sem[lsem]), [(cq, lo, hi), (cz, lo, hi)], lsem, 4 * q)
-        return 8 * q
+    def send(moves, rsem, lsem):
+        eng = shared(core, [T.cores[(s + m[0]) % N] for m in moves])
+        h = len(eng) // 2
+        calls = []
+        for i, (k, (x, a), (y, b), n) in enumerate(moves):
+            src, dst = A(x, a, a + n), A(y, b, b + n)
+            if x[1] == "q":
+                src, dst = src.bitcast(dt.uint8), dst.bitcast(dt.uint8)
+            calls.append(RemoteDMATransfer(dst_ids=[where(T.cores[(s + k) % N])], dma_engine_mask=mask(eng[h * i:h * i + h]),
+                                           remote_sem=T.sem[rsem], srcs=[src], dsts=[dst]))
+        remote(lambda: g.remote_dma_fused(calls, local_sem=T.sem[lsem]), [(x, a, a + n) for _, (x, a), _, n in moves], lsem, 2 * h)
+        return 2 * h
 
-    n1 = G * len(STAGES[0])
-    if len(STAGES) == 1:
-        gather("a", 2 * G, GT)
-        gather("v", 0, 2 * G)
-    else:
-        gather("a", n1 // 2, n1)
-        gather("v", 0, n1 // 2)
-        quant("cq", "cz", 0, "xb", SX // 4 + n1 - GT, GT)
-        n = send(STAGES[0], -1, "cq", "cz", G, lambda k: GT - n1 + G * (k - 1), lambda k: CL + G * (k - 1), "crecv0", "cloc")
-        arrives("crecv0", n, [(b, CL, CL + n1) for b in ("cq", "cz")])
-        if n1 < 2 * G:
-            gather("a", G, 2 * G)
-            gather("v", 2 * G, GT)
-        else:
-            gather("a", 2 * G, 3 * G)
-            gather("v", 3 * G, GT)
-    quant("cq", "cz", GT, "xb", SX // 4, GT)
-    for j, ks in enumerate(STAGES):
-        if j or len(STAGES) == 1:
-            n = send(ks, -1, "cq", "cz", G, lambda k: GT + G * (k - 1), lambda k: CL + G * (k - 1), "crecv%d" % j, "cloc")
-            arrives("crecv%d" % j, n, [(b, CL + G * (ks[0] - 1), CL + G * ks[-1]) for b in ("cq", "cz")])
+    gather("a", G, 2 * G)
+    gather("v", 0, G)
+    pick("v", ("ls16", 32, 64), ("fm", 0, 32), "off16", 2, 4, p4)
+    quant("cq", "cz", GT, "xb", SX // 4 - 2 * G, GT)
+    n = sum(send([(-k, (b, GT + G + G * k), (b, CL - G + G * k), G) for k in (1, 2)], "crecv0", "cloc") for b in ("cq", "cz"))
+    arrives("crecv0", n, [(b, CL, CL + 2 * G) for b in ("cq", "cz")])
+    gather("v", 2 * G, 3 * G)
+    gather("a", 3 * G, GT)
+    quant("cq", "cz", 0, "xb", SX // 4 - G, GT)
+    n = send([(-3, ("cq", GT - G), ("cq", CL + 2 * G), G), (-3, ("cz", GT - G), ("cz", CL + 2 * G), GT)], "crecv1", "cloc")
+    arrives("crecv1", n, [(b, CL + 2 * G, CL + 3 * G) for b in ("cq", "cz")])
+    quant("cq", "cz", 2 * GT, "xb", SX // 4, GT)
 
     def states(j):
-        if j >= len(STAGES):
-            return
-        ks = STAGES[j]
-        n = G * (len(ks) + (j == 0))
-        e = 4 * (GT - n1 + G * ks[-1])
+        n, e = (3 * G, 4 * GT) if j == 0 else (G, 4 * GT + 4 * G)
         for i in range(4):
-            mm("pa%d" % i, "aq", "az", 128 * i, "cq", "cz", CL + G * ks[-1] - GT, GT)
+            mm("pa%d" % i, "aq", "az", 128 * i, "cq", "cz", CL + (2 + j) * G - GT, GT)
         for i in range(4):
             o = ("hb", e - 4 * n + i, e, 4)
             r, w = [("pa%d" % i, 0, 512)], [("hb", 4 * j + i + 1, 4 * j + i + 2)]
@@ -424,83 +406,75 @@ def rank_program(g, core, T, topo):
                 emit("a", lambda: g.scalar.activation(ap(o), A("pa%d" % i, GT - n, GT), ACT.Relu, scale=0.05), r, w)
             else:
                 emit("v", lambda: g.vector.tensor_scalar(ap(o), A("pa%d" % i, GT - n, GT), 0.0, 0.05, ALU.max, ALU.mult), r, w)
-        a = GT * (j + 3 - len(STAGES))
+        a = GT * (1 - j)
         emit("v", lambda: g.vector.quantize_mx(A("hq", a, a + GT), A("hz", a, a + GT), A("hb", e - 4 * GT, e)),
              [("hb", 0, 4 * j + 5)], [("hq", a, a + GT), ("hz", a, a + GT)])
-        n = send(ks, 1, "hq", "hz", GB, lambda k: a + GT - GB - G * (ks[-1] - k), lambda k: HL + GB * (k - 1), "hrecv%d" % j, "hloc")
-        arrives("hrecv%d" % j, n, [(b, HL + GB * (ks[0] - 1), HL + GB * ks[-1]) for b in ("hq", "hz")])
+        if j == 0:
+            n = sum(send([(k, (b, 2 * GT - GB - G * (2 - k)), (b, HL + GB * (k - 1)), GB) for k in (1, 2)], "hrecv0", "hloc") for b in ("hq", "hz"))
+            arrives("hrecv0", n, [(b, HL, HL + 2 * GB) for b in ("hq", "hz")])
+        else:
+            n = send([(3, ("hq", GT - GB), ("hq", HL + 2 * GB), GB), (3, ("hz", GT - GB), ("hz", HL + 2 * GB), 4 * GB)], "hrecv1", "hloc")
+            arrives("hrecv1", n, [(b, HL + 2 * GB, HL + 3 * GB) for b in ("hq", "hz")])
 
     Y = ("msgin", 0, 1)
     if s > 1:
         Y = ("col", 0, 1)
         total(Y, ("msgin", 0, s), s)
-    left = [lambda: None] * 4
-    if s:
-        quant("bq", "bz", 16, "xb", XB // 4, 128)
-        mm("pl1", "pq", "pz", 16, "bq", "bz", 14, 128)
-        left = argmax("pl1", 0, 32, edge)
-        act(("be", 32, 64), ("zb", 0, 32), ("lr", 32, 33))
+    col = [("col", k, k + 1) for k in range(8)]
+    act(col[1], mine, Y if s else 0.0)
+    act(col[4], own, 159.0)
+    act(col[5], col[1], col[4], -1.0)
+    act(col[6], col[1], float(s + 1 + 159 + 1024))
+    act(col[5], col[5], -160.0)
+    act(col[7], nn, 161.0)
+    act(("lb1", 0, 32), ("cn", 0, 32), col[5], -1.0)
     act(("lb0", 0, 32), ("lr", 32, 64), 15.0, -1.0)
     quant("wq", "wz", 0, "wb", 0, 128)
     mm("pwx", "wq", "wz", 0, "xq", "xz", X0, 512)
     quant("aq", "az", 0, "ab", 0, 512)
-    left[0]()
-    nE = ("col", 1, 2)
-    ts(("u", 0, 32), ("cn", 0, 32), own, None, ALU.subtract)
-    left[1]()
-    if s:
-        ts(nE, nn, Y, 1.0, ALU.add, ALU.add)
-    else:
-        ts(nE, nn, 1.0, None, ALU.add)
-    left[2]()
+    emit("v", lambda: g.vector.tensor_scalar(A("in2", 0, 32), T.cn[:, 0:32].indirect(T.lg16[:, 4:6]), ap(col[4]), -1.0, ALU.subtract, ALU.mult),
+         [("cn", 0, 32), ("lg16", 4, 6), col[4]], [("in2", 0, 32)])
     quant("vq", "vz", 0, "vb", 0, 128)
-    left[3]()
-    if s:
-        act(("be", 0, 32), ("zb", 0, 32), ("bc", 15, 16))
-    cp(("wx", 0, 512), ("pwx", 0, 512), "a")
-    if len(STAGES) > 1:
-        states(0)
-    ts(("t1", 0, 16), ("u", 0, 16), pg[0], None, ALU.mult)
-    ts(("t2", 0, 16), ("u", 16, 32), pd16, None, ALU.mult)
-    ts(("lb1", 0, 32), ("u", 0, 32), nE, -1.0, ALU.add, ALU.mult)
-    tt(("in2", 0, 16), ("t1", 0, 16), ("t2", 0, 16), ALU.add)
-    tt(("in2", 16, 32), ("t1", 0, 16), ("t2", 0, 16), ALU.add)
-    if s:
-        tr(("br", 0, 64), ("be", 0, 64))
     tr(("ut", 0, 32), ("in2", 0, 32))
+    if s:
+        ts(col[3], true, nn, col[7], ALU.subtract, ALU.mult)
+    for d in range(2):
+        emit("v", lambda: g.vector.tensor_copy(T.wv[:, d:32:2], A("ut", 16 * d, 16 * d + 16)), [("ut", 0, 32)], [("wv", 16 * d, 16 * d + 16)])
+
     dma("s", "dl0", T.lb[0:1, :], T.lb0[0:16, :], [("lb0", 0, 32)], [])
     dma("s", "dl1", T.lb[1:2, :], T.lb1[0:16, :], [("lb1", 0, 32)], [])
-    if len(STAGES) == 1:
-        states(0)
+    states(0)
     states(1)
-    states(2)
+    cp(("wx", 0, YS), ("pwx", 0, YS), "a")
 
-    mm("pv", "vq", "vz", 0, "hq", "hz", 2 * GT, GT)
+    mm("pv", "vq", "vz", 0, "hq", "hz", 0, GT)
     cp(("hv", 2, GB), ("pv", 0, G), "a")
     cp(("hv", 0, 2), ("pv", GT - 2, GT), "a")
-    for d in range(2):
-        emit("v", lambda: g.vector.tensor_copy(T.wi[:, d:32:2], A("ut", 16 * d, 16 * d + 16)), [("ut", 0, 32)], [("wi", 16 * d, 16 * d + 16)])
-    ts(("wv", 0, 32), ("wi", 0, 32), -1.0, 159.0, ALU.mult, ALU.add)
-    ts(("zi", 0, 32), ("wi", 0, 32), nE, float(s + 1024), ALU.add, ALU.add)
+    ts(("zi", 0, 32), ("wv", 0, 32), -1.0, col[6], ALU.mult, ALU.add)
     ts(("ki", 0, 32), ("wv", 0, 32), 28, None, ALU.bitwise_and)
     ts(("kj", 0, 32), ("wv", 0, 32), 5, None, ALU.logical_shift_right)
-    if s:
-        ts(("cm", 0, 32), ("wi", 0, 32), nn, -1.0, ALU.add, ALU.is_equal)
-        ts(("col", 3, 4), ("br", 1, 2), ("br", 32, 33), -1.0, ALU.is_equal, ALU.mult)
-    tt(("gf", 0, 32), ("ki", 0, 32), ("kj", 0, 32), ALU.add)
     ts(("bi", 0, 32), ("zi", 0, 32), 3, None, ALU.bitwise_and)
+    tt(("gf", 0, 32), ("ki", 0, 32), ("kj", 0, 32), ALU.add)
     if s:
-        ts(("cm", 0, 32), ("cm", 0, 32), ("col", 3, 4), 1.0, ALU.mult, ALU.add)
+        ts(("cm", 0, 32), ("wv", 0, 32), 1.0, col[3], ALU.add, ALU.not_equal)
     ts(("bf", 0, 32), ("bi", 0, 32), float(GB), 1.0, ALU.mult, ALU.add)
     if s:
         tt(("gx", 0, 32), ("gf", 0, 32), ("cm", 0, 32), ALU.mult)
     tt(("ix", 0, 32), ("gx" if s else "gf", 0, 32), ("bf", 0, 32), ALU.add)
     cp(("ix16", 0, 32), ("ix", 0, 32))
 
+    mm("pl1", "vq", "vz", 0, "hq", "hz", HL + 2 * GB - 128, 128)
+    cp(("hv", GB, 3 * GB), ("pl1", 128 - 2 * GB, 128), "a")
     mm("pl0", "vq", "vz", 0, "hq", "hz", HL + 3 * GB - 128, 128)
-    cp(("hv", GB, 4 * GB), ("pl0", 128 - 3 * GB, 128))
-    for k, (c, d) in enumerate(((0, 160), (160, 352), (352, 512))):
-        emit("v", lambda: g.vector.tensor_tensor(A("yb", c, d), T.hv[:, 0:4 * GB].indirect(T.ix16[:, c // 16:d // 16]), A("wx", c, d), ALU.add),
-             [("hv", 0, 4 * GB), ("ix16", 0, 32), ("wx", c, d)], [("yb", c, d)])
-        dma("sas"[k], "dy%d" % k, T.y[:, c:d], A("yb", c, d), [("yb", c, d)], [])
+    cp(("hv", 3 * GB, 4 * GB), ("pl0", 128 - GB, 128))
+    pieces = ((0, YS), (YS, 384), (384, 512))
+    for c, d in pieces[1:]:
+        pick("a", ("wx", c, d), ("hv", 0, 4 * GB), "ix16", c // 16, d // 16)
+    for k, (c, d) in enumerate(pieces):
+        if c < YS:
+            emit("v", lambda: g.vector.tensor_tensor(A("yb", c, d), T.hv[:, 0:4 * GB].indirect(T.ix16[:, c // 16:d // 16]), A("wx", c, d), ALU.add),
+                 [("hv", 0, 4 * GB), ("ix16", 0, 32), ("wx", c, d)], [("yb", c, d)])
+        else:
+            tt(("yb", c, d), ("pwx", c, d), ("wx", c, d), ALU.add)
+        dma("ssa"[k], "dy%d" % k, T.y[:, c:d], A("yb", c, d), [("yb", c, d)], [])
     finish()

from concourse.bass import DstId, RemoteDMATransfer
from concourse.mybir import dt, AluOpType, ActivationFunctionType

ALU = AluOpType
ACT = ActivationFunctionType
N = 4
G = 32
GT = 4 * G
GB = G + 2
CL = 3 * GT
HL = 2 * GT
SX = 16 + 2048
X0 = 16
X1 = X0 + 512
XB = 16
BIG = 1e25
W0 = 32
FW = 800
TAB = 528
YS = 256
CC = 272

SCRATCH = {}
for _dtype, _names in {
    "bfloat16": "pb 64 pt 576 xb 2576 ab 2048 wb 512 vb 512 nn 256 cc 272 la 64 lr 64 msg 16 msgin 8 bn 48 bc 48 hb 640 tab 528 eb 512",
    "float32": "sc 256 rs 136 xm 264 eq 64 one 64 cn 128 nk 32 xa 32 rw 96 mt 16 sf 16 sm 16 bs 64 bx 64 be 64 pf 16 pg 16 l4 16 "
               "row 32 kn 8 kn2 8 kd 32 ji 128 jv 256 fw 800 fm 32 yj 64 col 16 in2 32 ut 32 gf 32 cm 32 gx 32 "
               "bf 32 ix 32 hv 136 wx 512 yb 512 lb0 32 lb1 32",
    "int32": "pi 12 wi 32 wv 32 zi 32 bi 32 ki 32 kj 32",
    "uint16": "lg16 16 of16 16 zi16 2 off16 16 ls16 64 ix16 32",
    "float8_e4m3fn_x4": "pq 144 xq 544 aq 512 wq 128 vq 128 cq 480 hq 360 nq 128",
    "uint8": "pz 144 xz 544 az 512 wz 128 vz 128 cz 576 hz 464 nz 128",
}.items():
    _l = _names.split()
    for _n, _w in zip(_l[::2], _l[1::2]):
        SCRATCH[_n] = ("sbuf", [128, int(_w)], _dtype)
SCRATCH["ft"] = ("sbuf", [128, 4, 32], "float32")
SCRATCH["fb"] = ("sbuf", [128, 8, 4], "float32")
for _n in ("pl0", "pl1", "pwx", "pa0", "pa1", "pa2", "pa3", "pv"):
    SCRATCH[_n] = ("psum", [128, 512], "float32")
SEMAPHORES = ["sv", "sa", "st", "sg", "lrecv", "rrecv", "bnq", "mrecv0", "mrecv1", "mrecv2", "mloc", "crecv0", "crecv1", "cloc", "hrecv0", "hrecv1", "hloc",
              "dp", "de", "dx0", "dx1", "dx2", "dx3", "da", "dw", "dv", "dl0", "dl1", "dy0", "dy1", "dy2"]


def tracker(g, T):
    queues = {"v": g.vector, "a": g.scalar, "t": g.tensor, "g": g, "s": g.sync}
    know = {q: {} for q in queues}
    count = {}
    acc = {}
    order = [0]

    def wait(q, tok):
        sem, n, snap = tok
        if know[q].get(sem, 0) < n:
            queues[q].wait_ge(T.sem[sem], n)
            for k, v in snap.items():
                if know[q].get(k, 0) < v:
                    know[q][k] = v
            know[q][sem] = max(n, know[q].get(sem, 0))

    def settle(q, reads, writes):
        deps = []
        for buf, a, b in reads:
            deps += [(o, tok) for (c, d, w, tok, o) in acc.get(buf, []) if w and a < d and c < b]
        for buf, a, b in writes:
            deps += [(o, tok) for (c, d, w, tok, o) in acc.get(buf, []) if a < d and c < b]
        for o, tok in sorted(deps, key=lambda z: -z[0]):
            wait(q, tok)

    def note(tok, reads, writes):
        order[0] += 1
        for buf, a, b in reads:
            acc.setdefault(buf, []).append((a, b, False, tok, order[0]))
        for buf, a, b in writes:
            acc.setdefault(buf, []).append((a, b, True, tok, order[0]))

    def emit(q, call, reads, writes, sem=None, inc=1, chain=False):
        settle(q, reads, [] if chain else writes)
        sem = sem or "s" + q
        call().then_inc(T.sem[sem], inc)
        count[sem] = count.get(sem, 0) + inc
        note((sem, count[sem], dict(know[q])), reads, writes)

    def remote(call, reads, sem, n):
        settle("g", reads, [])
        call()
        count[sem] = count.get(sem, 0) + n

    def arrives(sem, n, writes):
        count[sem] = count.get(sem, 0) + n
        note((sem, n, {}), [], writes)

    def finish():
        for sem, n in count.items():
            wait("g", (sem, n, {}))

    return emit, remote, arrives, finish


def rank_program(g, core, T, topo):
    s = T.rank_of(core)
    if s is None:
        return
    emit, remote, arrives, finish = tracker(g, T)

    def A(name, a, b):
        return T[name][:, a:b]

    def span(t):
        return ("eb", t[1] + 32, t[2] + 32) if t[0] == "zb" else (t[0], t[1], t[2])

    def ap(t):
        return T[t[0]][:, t[1]:t[2]:t[3]] if len(t) > 3 else A(*span(t))

    def dma(q, sem, out, in_, reads, writes):
        eng = g.sync if q == "s" else g.scalar
        emit(q, lambda: eng.dma_start(out, in_), reads, writes, sem=sem, inc=16)

    def tt(o, x, y, op):
        emit("v", lambda: g.vector.tensor_tensor(ap(o), ap(x), ap(y), op), [span(x), span(y)], [span(o)])

    def ts(o, x, s1, s2, op0, op1=None):
        r = [span(x)] + [span(z) for z in (s1, s2) if isinstance(z, tuple)]
        c1 = ap(s1) if isinstance(s1, tuple) else s1
        c2 = ap(s2) if isinstance(s2, tuple) else s2
        if op1 is None:
            emit("v", lambda: g.vector.tensor_scalar(ap(o), ap(x), c1, None, op0), r, [span(o)])
        else:
            emit("v", lambda: g.vector.tensor_scalar(ap(o), ap(x), c1, c2, op0, op1), r, [span(o)])

    def cp(o, x, q="v"):
        if q == "v":
            emit("v", lambda: g.vector.tensor_copy(ap(o), ap(x)), [span(x)], [span(o)])
        else:
            emit("a", lambda: g.scalar.activation(ap(o), ap(x), ACT.Copy), [span(x)], [span(o)])

    def act(o, x, bias, scale=1.0, f=ACT.Identity):
        r = [span(x)] + ([span(bias)] if isinstance(bias, tuple) else [])
        b = ap(bias) if isinstance(bias, tuple) else bias
        emit("a", lambda: g.scalar.activation(ap(o), ap(x), f, bias=b, scale=scale), r, [span(o)])

    def total(o, x, n):
        emit("a", lambda: g.scalar.activation(A("yj", 0, n), ap(x), ACT.Copy, accum_out=ap(o)), [span(x)], [("yj", 0, n), span(o)])

    def fill(o, c):
        emit("v", lambda: g.vector.memset(ap(o), c), [], [span(o)])

    def tr(o, x):
        emit("v", lambda: g.vector.transpose(ap(o), ap(x)), [span(x)], [span(o)])

    def scan(o, d0, d1, init, op0, op1):
        r = [span(d0), span(d1)] + ([span(init)] if isinstance(init, tuple) else [])
        c = ap(init) if isinstance(init, tuple) else init
        emit("v", lambda: g.vector.tensor_tensor_scan(ap(o), ap(d0), ap(d1), c, op0, op1), r, [span(o)])

    def quant(cq, cz, a, src, b, n):
        emit("v", lambda: g.vector.quantize_mx(A(cq, a, a + n), A(cz, a, a + n), A(src, 4 * b, 4 * b + 4 * n)),
             [(src, 4 * b, 4 * b + 4 * n)], [(cq, a, a + n), (cz, a, a + n)])

    def mm(o, lq, lz, a, rq, rz, b, n, start=True, stop=True):
        emit("t", lambda: g.tensor.matmul_mx(A(o, 0, n), A(lq, a, a + 128), A(lz, a, a + 128), A(rq, b, b + n), A(rz, b, b + n), start, stop),
             [(lq, a, a + 128), (lz, a, a + 128), (rq, b, b + n), (rz, b, b + n)], [(o, 0, 512)], chain=not start)

    def iota(o, pattern, base, cm=0):
        if o[0] == "pi":
            emit("g", lambda: g.iota(ap(o), pattern, base, cm), [], [span(o)])
        else:
            emit("g", lambda: g.iota(ap(o), pattern, base, cm, allow_small_or_imprecise_dtypes=True), [], [span(o)])

    def pick(q, o, win, off, a, b, plus=None, c=0.0):
        w = ap(win).indirect(T[off][:, a:b])
        r = [span(win), (off, a, b)]
        if plus:
            emit("v", lambda: g.vector.tensor_scalar(ap(o), w, ap(plus), c, ALU.add, ALU.add), r + [span(plus)], [span(o)])
        elif q == "v":
            emit("v", lambda: g.vector.tensor_copy(ap(o), w), r, [span(o)])
        else:
            emit("a", lambda: g.scalar.activation(ap(o), w, ACT.Copy), r, [span(o)])

    def shared(src, dsts):
        return [e for e in topo.engines(src, dsts[0]) if all(e in topo.engines(src, d) for d in dsts)]

    def mask(engines):
        return sum(1 << e for e in engines)

    def where(d):
        rid, pid, _ = topo.addr(d)
        return DstId(rid=rid, pnc=pid)

    dma("a", "dp", A("pb", 0, 64), T.p[:, 0:64], [], [("pb", 0, 64)])
    dma("s", "de", A("eb", 24, 32), T.x[:, 0:8] if s == N - 1 else T.x[:, 2040:2048], [], [("eb", 24, 32)])
    for k, que in enumerate("sasa"):
        c = XB + 512 * k
        dma(que, "dx%d" % k, A("xb", c, c + 512), T.x[:, 512 * k:512 * k + 512], [], [("xb", c, c + 512)])
    for n, w in (("a", 2048), ("w", 512), ("v", 512)):
        dma("s", "d" + n, A(n + "b", 0, w), T[n][:, 0:w], [], [(n + "b", 0, w)])

    iota(("pi", 0, 2), [[-15, 2]], 15, 1)
    iota(("row", 0, 16), [[1, 16]], 0)
    iota(("ji", 0, 128), [[4, 8], [128, 16]], 0)
    iota(("kd", 0, 32), [[1, 32]], 129)
    fill(("eb", 32, 512), 0.0)
    fill(("eb", 0, 24), 0.0)
    fill(("pt", 0, 576), 0.0)
    act(("rs", 0, 136), ("zb", 0, 136), BIG)
    for o, c in ((2, 15), (4, 3)):
        ts(("pi", o, o + 2), ("pi", 0, 2), c, None, ALU.bitwise_and)
    for o, c, d in ((6, 2, 3), (8, 3, 1), (10, 4, 1)):
        ts(("pi", o, o + 2), ("pi", 0, 2), c, d, ALU.logical_shift_right, ALU.bitwise_and)
    cp(("pf", 0, 10), ("pi", 2, 12))

    def border(d, xq, a, xz, za, bq, b, bz, zb, rsem):
        e = shared(core, [d])
        h = len(e) // 2
        moves = [RemoteDMATransfer(dst_ids=[where(d)], dma_engine_mask=mask(e[:h]), remote_sem=T.sem[rsem],
                                   srcs=[A(xq, a, a + 2).bitcast(dt.uint8)], dsts=[A(bq, b, b + 2).bitcast(dt.uint8)]),
                 RemoteDMATransfer(dst_ids=[where(d)], dma_engine_mask=mask(e[h:]), remote_sem=T.sem[rsem],
                                   srcs=[A(xz, za, za + 8)], dsts=[A(bz, zb, zb + 8)])]
        remote(lambda: g.remote_dma_fused(moves, local_sem=T.sem["b" + xq]), [(xq, a, a + 2), (xz, za, za + 8)], "b" + xq, len(e))
        return len(e)

    quant("nq", "nz", 0, "eb", 0, 128)
    if s == N - 1:
        border(T.cores[s - 1], "nq", 5, "nz", 5, "xq", X1, "xz", X1, "rrecv")
    else:
        border(T.cores[s + 1], "nq", 6, "nz", 0, "xq", X0 - 2, "xz", X0 - 8, "lrecv")
    iota(("tab", 0, TAB), [[0, TAB // 4], [-1, 4]], 3)
    for k in range(4):
        cp(("pt", 64 + 128 * k, 128 + 128 * k), ("pb", 0, 64), "va"[k // 2])
    act(("rs", 0, 136, 16), ("zb", 0, 9), -BIG)
    act(("xm", 0, 1), ("zb", 0, 1), -BIG)
    act(("bx", 0, 64), ("zb", 0, 64), -BIG)

    def argmax(pl, c, n, bufs):
        sc, xm, nn_, cc, o, w = bufs
        return [lambda: tr((sc, o, o + n), (pl, c, c + n)),
                lambda: scan((xm, o + 1, o + w + 1), (sc, o, o + w), ("rs", 1, w + 1), -BIG, ALU.max, ALU.min),
                lambda: tt((nn_, o, o + w), (sc, o, o + w), (xm, o, o + w), ALU.is_le),
                lambda: scan((cc, o, o + w), (nn_, o, o + w), (nn_, o, o + w), 0.0, ALU.mult, ALU.add)]

    def quarter(c):
        quant("xq", "xz", X0 + 128 * c, "xb", XB // 4 + 128 * c, 128)

    def score(c):
        mm("pl%d" % (c // 2), "pq", "pz", 16 - 16 * (c % 2), "xq", "xz", X0 + 128 * c, 128, c % 2 == 0, c % 2 == 1)

    half0 = argmax("pl0", 0, 128, ("sc", "xm", "nn", "cc", 0, 128))
    half1 = argmax("pl1", 0, 128, ("sc", "xm", "nn", "cc", 128, 128))
    guests = [("pv", 1, 2)] * (s > 0) + [("pwx", 127, 128)] * (s == N - 2)

    quarter(0)
    quant("pq", "pz", 0, "pt", 0, 144)
    score(0)
    quarter(1)
    score(1)
    p16, p4, pd4, pd8, pd16 = [("pf", k, k + 1) for k in (1, 3, 5, 7, 9)]
    pg = [("pg", k, k + 1) for k in range(16)]
    act(("cc", 256, CC), ("zb", 0, CC - 256), -1.0)
    act(("one", 0, 64), ("zb", 0, 64), 1.0)
    act(("eq", 32, 64), ("zb", 0, 32), 1.0)
    act(pg[8], p16, 1.0, -1.0, ACT.Relu)
    act(pg[3], ("pf", 3, 4), 15.0, 32.0)
    act(pg[8], pg[8], 15.0)
    act(pg[5], ("pf", 5, 6), pg[3], 16.0)
    act(pg[2], ("pf", 2, 3), pg[8], 32.0)
    act(pg[7], ("pf", 7, 8), pg[5], 96.0)
    act(pg[4], ("pf", 4, 5), pg[2], 16.0)
    act(("l4", 2, 4), ("zb", 0, 2), pg[7])
    act(pg[6], ("pf", 6, 7), pg[4], 96.0)
    act(pg[1], pd16, p16, 16.0)
    act(("l4", 0, 2), ("zb", 0, 2), pg[6])
    act(pg[9], p16, 0.0, 32.0)
    act(("l4", 4, 6), ("zb", 0, 2), pg[1])
    act(("kd", 0, 32), ("kd", 0, 32), pg[9])
    act(("sm", 0, 16), ("row", 0, 16), p16, -1.0, ACT.Sign)
    act(pg[14], pd16, 0.0, 64.0)
    act(("sm", 0, 16), ("sm", 0, 16), 0.0, 1.0, ACT.Abs)
    act(pg[15], pd16, 32.0, 64.0)
    act(("fw", W0, W0 + 128), ("zb", 0, 128), 0.0)
    for k in range(2):
        act(("jv", 128 * k, 128 * k + 128), ("ji", 0, 128), pg[14 + k])
    quarter(2)
    score(2)
    quarter(3)
    score(3)
    half0[0]()
    if s:
        arrives("lrecv", len(shared(T.cores[s - 1], [core])), [("xq", X0 - 2, X0), ("xz", X0 - 8, X0)])
        mm("pv", "pq", "pz", 16, "xq", "xz", X0 - 2, 128)
    if s == N - 2:
        arrives("rrecv", len(shared(T.cores[s + 1], [core])), [("xq", X1, X1 + 2), ("xz", X1, X1 + 8)])
        mm("pwx", "pq", "pz", 16, "xq", "xz", X1 + 2 - 128, 128)
    half0[1]()
    half1[0]()
    half0[2]()
    half1[1]()
    half0[3]()
    half1[2]()
    cp(("lg16", 0, 6), ("l4", 0, 6))
    half1[3]()

    later = sorted((T.cores[d] for d in range(N - 1, s, -1)), key=lambda d: topo.same_plane(topo.chip(core), topo.chip(d)))
    pick("v", ("la", 0, 64), ("cc", 0, CC), "lg16", 0, 4)
    tr(("lr", 0, 64), ("la", 0, 64))
    ng = len(guests)
    for k, c in enumerate(guests):
        ts(("be", 32 * k, 32 * k + 32), ("zb", 0, 32), c, None, ALU.subtract)
        act(("cn", 64 + 32 * k, 96 + 32 * k), ("zb", 0, 32), ("lr", 32 + 31 * k, 33 + 31 * k))
    tt(("eq", 0, 32), ("lr", 32, 64), ("lr", 31, 63), ALU.is_equal)
    if ng:
        tr(("bs", 0, 32 * ng), ("be", 0, 32 * ng))
    scan(("cn", 0, 64), ("eq", 0, 64), ("one", 0, 64), 0.0, ALU.add, ALU.subtract)
    for k in range(ng):
        c = 32 * k
        scan(("bx", c, c + 16), ("bs", c, c + 16), ("bs", c, c + 16), BIG, ALU.min, ALU.min)
        emit("a", lambda: g.scalar.activation(A("yj", c, c + 31), A("bx", c, c + 31), ACT.Sign, bias=A("bx", c + 15, c + 16), scale=-1.0,
                                              accum_out=A("col", 9 + k, 10 + k)), [("bx", c, c + 31)], [("yj", c, c + 31), ("col", 9 + k, 10 + k)])
    tr(("rw", 0, 32 + 32 * ng), ("cn", 32, 64 + 32 * ng))
    tt(("nk", 0, 32), ("eq", 0, 32), ("kd", 0, 32), ALU.mult)
    nn = ("mt", 15, 16)
    own = ("sf", 15, 16)
    msg = ("msg", 15, 16)
    true = msg if s < 2 else ("col", 8, 9)
    scan(("mt" if s else "msg", 0, 16), ("rw", 0, 16), ("zb", 0, 16), 0.0, ALU.add, ALU.add)
    if s == 0:
        nn = msg
    scan(("sf", 0, 16), ("sm", 0, 16), ("rw", 0, 16), 0.0, ALU.mult, ALU.add)
    if s:
        ts(true, ("col", 9, 10), ("rw", 32, 33), nn, ALU.is_equal, ALU.add)
    tt(("xa", 0, 32), ("nk", 0, 32), ("cn", 0, 32), ALU.subtract)
    if s == N - 2:
        ts(msg, ("col", 10, 11), ("rw", 79, 80), true, ALU.is_equal, ALU.add)
    pick("v", ("of16", 0, 16), ("xa", 0, 32), "lg16", 4, 5, own, float(W0 + 127))
    mine = nn if s == N - 1 else true
    if later:
        eng = shared(core, later)
        remote(lambda: g.remote_dma_fused([RemoteDMATransfer(dst_ids=[where(d) for d in later], dma_engine_mask=mask(eng), remote_sem=T.sem["mrecv%d" % s],
                                                             srcs=[A("msg", 15, 16)], dsts=[A("msgin", s, s + 1) for _ in later])],
                                          local_sem=T.sem.mloc), [("msg", 15, 16)], "mloc", len(eng))
    for r in range(s):
        arrives("mrecv%d" % r, len(shared(T.cores[r], T.cores[r + 1:])), [("msgin", r, r + 1)])
    act(("kn", 0, 1), p4, float(N - s))
    act(pg[10], p16, 0.0, 4.0)
    act(("kn2", 0, 1), mine, ("kn", 0, 1), -1.0)
    act(pg[11], pd8, pg[10], -32.0)
    emit("a", lambda: g.scalar.activation(A("hb", 0, 4 * G), ap(("zb", 0, 4 * G)), ACT.Copy), [span(("zb", 0, 4 * G))], [("hb", 0, 1)])
    emit("v", lambda: g.vector.tensor_copy(T.fw[:, 0:FW].indirect(T.of16[:, 0:16]), A("jv", 0, 256)),
         [("jv", 0, 256), ("of16", 0, 16)], [("fw", 0, FW)])
    emit("v", lambda: g.vector.transpose(T.ft[:, :, :], A("fw", W0, W0 + 128)), [("fw", W0, W0 + 128)], [("ft", 0, 128)])
    m = [("msgin", r, r + 1) for r in range(s)]
    z = ("kn2", 0, 1)
    for h in range(2):
        emit("v", lambda: g.vector.tensor_tensor(T.fb[:, 4 * h:4 * h + 4, :], T.ft[:, :, 0:4], T.ft[:, :, 16:20], ALU.max),
             [("ft", 0, 128)], [("fb", 16 * h, 16 * h + 16)])
    if s == 3:
        act(("kn2", 1, 2), m[0], z, -1.0)
        z, m = ("kn2", 1, 2), m[1:]
    if len(m) == 2:
        ts(("zi16", 0, 1), z, m[0], m[1], ALU.subtract, ALU.subtract)
    elif m:
        ts(("zi16", 0, 1), z, m[0], None, ALU.subtract)
    else:
        cp(("zi16", 0, 1), z)
    emit("v", lambda: g.vector.transpose(A("fm", 0, 32), T.fb[:, :, :]), [("fb", 0, 32)], [("fm", 0, 32)])
    pick("v", ("off16", 0, 16), ("tab", 0, TAB), "zi16", 0, 1, pg[11])
    pick("v", ("ls16", 0, 32), ("fm", 0, 32), "off16", 0, 2, p4)

    def gather(q, a, b):
        c = 8 + a // 4 + 16 * (a >= 2 * G)
        pick(q, ("xb", SX + 4 * a, SX + 4 * b), ("xb", XB, SX), "ls16", c, c + (b - a) // 4)

    def send(moves, rsem, lsem):
        eng = shared(core, [T.cores[(s + m[0]) % N] for m in moves])
        h = len(eng) // 2
        calls = []
        for i, (k, (x, a), (y, b), n) in enumerate(moves):
            src, dst = A(x, a, a + n), A(y, b, b + n)
            if x[1] == "q":
                src, dst = src.bitcast(dt.uint8), dst.bitcast(dt.uint8)
            calls.append(RemoteDMATransfer(dst_ids=[where(T.cores[(s + k) % N])], dma_engine_mask=mask(eng[h * i:h * i + h]),
                                           remote_sem=T.sem[rsem], srcs=[src], dsts=[dst]))
        remote(lambda: g.remote_dma_fused(calls, local_sem=T.sem[lsem]), [(x, a, a + n) for _, (x, a), _, n in moves], lsem, 2 * h)
        return 2 * h

    gather("a", G, 2 * G)
    gather("v", 0, G)
    pick("v", ("ls16", 32, 64), ("fm", 0, 32), "off16", 2, 4, p4)
    quant("cq", "cz", GT, "xb", SX // 4 - 2 * G, GT)
    n = sum(send([(-k, (b, GT + G + G * k), (b, CL - G + G * k), G) for k in (1, 2)], "crecv0", "cloc") for b in ("cq", "cz"))
    arrives("crecv0", n, [(b, CL, CL + 2 * G) for b in ("cq", "cz")])
    gather("v", 2 * G, 3 * G)
    gather("a", 3 * G, GT)
    quant("cq", "cz", 0, "xb", SX // 4 - G, GT)
    n = send([(-3, ("cq", GT - G), ("cq", CL + 2 * G), G), (-3, ("cz", GT - G), ("cz", CL + 2 * G), GT)], "crecv1", "cloc")
    arrives("crecv1", n, [(b, CL + 2 * G, CL + 3 * G) for b in ("cq", "cz")])
    quant("cq", "cz", 2 * GT, "xb", SX // 4, GT)

    def states(j):
        n, e = (3 * G, 4 * GT) if j == 0 else (G, 4 * GT + 4 * G)
        for i in range(4):
            mm("pa%d" % i, "aq", "az", 128 * i, "cq", "cz", CL + (2 + j) * G - GT, GT)
        for i in range(4):
            o = ("hb", e - 4 * n + i, e, 4)
            r, w = [("pa%d" % i, 0, 512)], [("hb", 4 * j + i + 1, 4 * j + i + 2)]
            if i % 2 == 0:
                emit("a", lambda: g.scalar.activation(ap(o), A("pa%d" % i, GT - n, GT), ACT.Relu, scale=0.05), r, w)
            else:
                emit("v", lambda: g.vector.tensor_scalar(ap(o), A("pa%d" % i, GT - n, GT), 0.0, 0.05, ALU.max, ALU.mult), r, w)
        a = GT * (1 - j)
        emit("v", lambda: g.vector.quantize_mx(A("hq", a, a + GT), A("hz", a, a + GT), A("hb", e - 4 * GT, e)),
             [("hb", 0, 4 * j + 5)], [("hq", a, a + GT), ("hz", a, a + GT)])
        if j == 0:
            n = sum(send([(k, (b, 2 * GT - GB - G * (2 - k)), (b, HL + GB * (k - 1)), GB) for k in (1, 2)], "hrecv0", "hloc") for b in ("hq", "hz"))
            arrives("hrecv0", n, [(b, HL, HL + 2 * GB) for b in ("hq", "hz")])
        else:
            n = send([(3, ("hq", GT - GB), ("hq", HL + 2 * GB), GB), (3, ("hz", GT - GB), ("hz", HL + 2 * GB), 4 * GB)], "hrecv1", "hloc")
            arrives("hrecv1", n, [(b, HL + 2 * GB, HL + 3 * GB) for b in ("hq", "hz")])

    Y = ("msgin", 0, 1)
    if s > 1:
        Y = ("col", 0, 1)
        total(Y, ("msgin", 0, s), s)
    col = [("col", k, k + 1) for k in range(8)]
    act(col[1], mine, Y if s else 0.0)
    act(col[4], own, 159.0)
    act(col[5], col[1], col[4], -1.0)
    act(col[6], col[1], float(s + 1 + 159 + 1024))
    act(col[5], col[5], -160.0)
    act(col[7], nn, 161.0)
    act(("lb1", 0, 32), ("cn", 0, 32), col[5], -1.0)
    act(("lb0", 0, 32), ("lr", 32, 64), 15.0, -1.0)
    quant("wq", "wz", 0, "wb", 0, 128)
    mm("pwx", "wq", "wz", 0, "xq", "xz", X0, 512)
    quant("aq", "az", 0, "ab", 0, 512)
    emit("v", lambda: g.vector.tensor_scalar(A("in2", 0, 32), T.cn[:, 0:32].indirect(T.lg16[:, 4:6]), ap(col[4]), -1.0, ALU.subtract, ALU.mult),
         [("cn", 0, 32), ("lg16", 4, 6), col[4]], [("in2", 0, 32)])
    quant("vq", "vz", 0, "vb", 0, 128)
    tr(("ut", 0, 32), ("in2", 0, 32))
    if s:
        ts(col[3], true, nn, col[7], ALU.subtract, ALU.mult)
    for d in range(2):
        emit("v", lambda: g.vector.tensor_copy(T.wv[:, d:32:2], A("ut", 16 * d, 16 * d + 16)), [("ut", 0, 32)], [("wv", 16 * d, 16 * d + 16)])

    dma("s", "dl0", T.lb[0:1, :], T.lb0[0:16, :], [("lb0", 0, 32)], [])
    dma("s", "dl1", T.lb[1:2, :], T.lb1[0:16, :], [("lb1", 0, 32)], [])
    states(0)
    states(1)
    cp(("wx", 0, YS), ("pwx", 0, YS), "a")

    mm("pv", "vq", "vz", 0, "hq", "hz", 0, GT)
    cp(("hv", 2, GB), ("pv", 0, G), "a")
    cp(("hv", 0, 2), ("pv", GT - 2, GT), "a")
    ts(("zi", 0, 32), ("wv", 0, 32), -1.0, col[6], ALU.mult, ALU.add)
    ts(("ki", 0, 32), ("wv", 0, 32), 28, None, ALU.bitwise_and)
    ts(("kj", 0, 32), ("wv", 0, 32), 5, None, ALU.logical_shift_right)
    ts(("bi", 0, 32), ("zi", 0, 32), 3, None, ALU.bitwise_and)
    tt(("gf", 0, 32), ("ki", 0, 32), ("kj", 0, 32), ALU.add)
    if s:
        ts(("cm", 0, 32), ("wv", 0, 32), 1.0, col[3], ALU.add, ALU.not_equal)
    ts(("bf", 0, 32), ("bi", 0, 32), float(GB), 1.0, ALU.mult, ALU.add)
    if s:
        tt(("gx", 0, 32), ("gf", 0, 32), ("cm", 0, 32), ALU.mult)
    tt(("ix", 0, 32), ("gx" if s else "gf", 0, 32), ("bf", 0, 32), ALU.add)
    cp(("ix16", 0, 32), ("ix", 0, 32))

    mm("pl1", "vq", "vz", 0, "hq", "hz", HL + 2 * GB - 128, 128)
    cp(("hv", GB, 3 * GB), ("pl1", 128 - 2 * GB, 128), "a")
    mm("pl0", "vq", "vz", 0, "hq", "hz", HL + 3 * GB - 128, 128)
    cp(("hv", 3 * GB, 4 * GB), ("pl0", 128 - GB, 128))
    pieces = ((0, YS), (YS, 384), (384, 512))
    for c, d in pieces[1:]:
        pick("a", ("wx", c, d), ("hv", 0, 4 * GB), "ix16", c // 16, d // 16)
    for k, (c, d) in enumerate(pieces):
        if c < YS:
            emit("v", lambda: g.vector.tensor_tensor(A("yb", c, d), T.hv[:, 0:4 * GB].indirect(T.ix16[:, c // 16:d // 16]), A("wx", c, d), ALU.add),
                 [("hv", 0, 4 * GB), ("ix16", 0, 32), ("wx", c, d)], [("yb", c, d)])
        else:
            tt(("yb", c, d), ("pwx", c, d), ("wx", c, d), ALU.add)
        dma("ssa"[k], "dy%d" % k, T.y[:, c:d], A("yb", c, d), [("yb", c, d)], [])
    finish()
